import numpy as np
import ml_dtypes


def mxq(x, axis, fmt="e4m3"):
    dtype, down = {"e4m3": (ml_dtypes.float8_e4m3fn, 7), "e5m2": (ml_dtypes.float8_e5m2, 14)}[fmt]
    v = np.moveaxis(np.asarray(x, np.float32).astype(ml_dtypes.bfloat16).astype(np.float64), axis, -1)
    blocks = v.reshape(v.shape[:-1] + (-1, 32))
    amax = np.abs(blocks).max(-1, keepdims=True)
    byte = np.maximum(np.where(amax > 0, np.frexp(amax)[1] - 1 + 127, 0) - down, 1)
    scale = np.exp2(byte - 127.0)
    codes = (blocks / scale).astype(np.float32).astype(dtype).astype(np.float64)
    return np.moveaxis((codes * scale).reshape(v.shape), -1, axis)


WIDE = False


def mx_kscale(k):
    if not WIDE:
        return np.ones(k)
    levels = np.array([10, -10, 5, -5, 0])
    if k % 512:
        return np.exp2(np.random.permutation(np.resize(levels, k // 32))).repeat(32)
    a = np.empty((k // 512, 16))
    for p in range(k // 512):
        a[p, :8] = np.random.permutation(np.resize(levels, 8))
        for g in range(8):
            far = levels[np.abs(levels - a[p, g]) >= 10]
            a[p, g + 8] = far[np.random.randint(len(far))]
    return np.exp2(a.ravel()).repeat(32)


BF16 = ml_dtypes.bfloat16


def bf(x):
    return np.asarray(x, np.float32).astype(BF16)


def f64(x):
    return np.asarray(x).astype(np.float64)


E2M1 = np.array([0.0, 0.5, 1.0, 1.5, 2.0, 3.0, 4.0, 6.0, -0.0, -0.5, -1.0, -1.5, -2.0, -3.0, -4.0, -6.0])


def pack_weight(w, fmt):
    k, n = w.shape
    w = f64(bf(w)).reshape(k // 32, 32, n)
    amax = np.abs(w).max(1)
    if fmt == "e4m3":
        byte = np.frexp(amax)[1] - 1 + 127 - 7
    else:
        mant, ex = np.frexp(amax / 6.0)
        byte = np.where(mant > 0.5, ex, ex - 1) + 127
    byte = np.clip(np.where(amax > 0, byte, 1), 1, 254)
    scaled = (w * np.exp2(127.0 - byte)[:, None, :]).reshape(k, n).astype(np.float32)
    by_word = np.ascontiguousarray(scaled.reshape(k // 512, 128, 4, n).transpose(0, 1, 3, 2))
    if fmt == "e4m3":
        words = by_word.astype(ml_dtypes.float8_e4m3fn).view(np.uint8)
    else:
        c = by_word.astype(ml_dtypes.float4_e2m1fn).view(np.uint8) & 0xF
        words = c[..., 0::2] | (c[..., 1::2] << 4)
    return np.ascontiguousarray(words), np.ascontiguousarray(byte.astype(np.uint8).reshape(k // 512, 16, n))


def unpack_weight(words, scales, fmt):
    g, p, n, _ = words.shape
    if fmt == "e4m3":
        vals = np.ascontiguousarray(words).view(ml_dtypes.float8_e4m3fn).astype(np.float64)
    else:
        nib = np.empty((g, p, n, 4), np.uint8)
        nib[..., 0::2] = words & 0xF
        nib[..., 1::2] = words >> 4
        vals = E2M1[nib]
    vals = vals * np.repeat(np.exp2(scales.astype(np.float64) - 127.0), 8, axis=1)[..., None]
    return vals.transpose(0, 1, 3, 2).reshape(g * 512, n)
def pack4(w):
    words, scales = pack_weight(w, "e2m1")
    return words.reshape(words.shape[0], 128, -1), scales


def unpack4(words, scales):
    return unpack_weight(words.reshape(words.shape[0], 128, -1, 2), scales, "e2m1")


def planes(Y):
    n, m = Y.shape
    b = f64(bf(Y)).reshape(n // 32, 32, m)
    amax = np.abs(b).max(1)
    byte = np.clip(np.where(amax > 0, np.frexp(amax)[1] - 1 + 127 - 7, 1), 1, 254)
    codes = (b * np.exp2(127.0 - byte)[:, None, :]).reshape(n, m).astype(np.float32).astype(ml_dtypes.float8_e4m3fn).view(np.uint8)
    words = codes.reshape(n // 512, 128, 4, m).transpose(0, 1, 3, 2)
    return np.ascontiguousarray(words), np.ascontiguousarray(byte.astype(np.uint8).reshape(n // 512, 16, m))


G, T, K, D, V = 4, 1024, 1024, 512, 1024
BETA = 0.9

def setup_inputs():
    s, t = mx_kscale(K), mx_kscale(T)
    x = np.random.randn(T, K) * s[None, :]
    a = np.random.randn(G, K, D) / np.sqrt(K) / s[None, :, None]
    a_words, a_scales = pack4(a.reshape(G * K, D))
    z = 2.0 * np.random.randn(G, T, V)
    e = np.exp(z - z.max(axis=2, keepdims=True))
    prob = e / e.sum(axis=2, keepdims=True)
    u = z - np.log(np.random.exponential(1.0, (G, T, V)))
    err = prob - (u >= u.max(axis=2, keepdims=True))
    return {
        "x": bf(x),
        "a_words": a_words,
        "a_scales": a_scales,
        "bias": bf(0.3 * np.random.randn(G, D)),
        "token_weight": bf(np.exp(0.3 * np.random.randn(G, T)) * t[None, :]),
        "err": bf(err / t[None, :, None]),
        "running": bf(0.5 * np.random.randn(G, D, V)),
        "rate": bf(np.exp(0.8 * np.random.randn(G, V))),
    }

def reference(x, a_words, a_scales, bias, token_weight, err, running, rate):
    A = unpack4(a_words, a_scales).reshape(G, K, D)
    X = mxq(f64(x), 1)
    H = ((X @ A) + f64(bias)[:, None, :]) * f64(token_weight)[:, :, None]
    grad = mxq(H, 1).swapaxes(1, 2) @ mxq(f64(err), 1)
    y = (BETA * f64(running) + grad) * f64(rate)[:, None, :]
    Y = y.reshape(G * D, V).T
    words, scales = planes(Y)
    return y, words, scales

@@ -1,0 +1,405 @@
+from contextlib import ExitStack
+
+import concourse.mybir as mybir
+from concourse.masks import make_identity
+
+G, T, K, D, V = 4, 1024, 1024, 512, 1024
+BETA = 0.9
+FLOPS = 2 * G * (T * K * D + T * D * V)
+
+F32 = mybir.dt.float32
+BF16 = mybir.dt.bfloat16
+I32 = mybir.dt.int32
+U32 = mybir.dt.uint32
+U8 = mybir.dt.uint8
+FP8X4 = mybir.dt.float8_e4m3fn_x4
+FP4X4 = mybir.dt.float4_e2m1fn_x4
+ADD = mybir.AluOpType.add
+MULT = mybir.AluOpType.mult
+
+P = 128
+PASS = 512
+BANK = 512
+TILES = D // P
+UNITS = G * TILES
+LEAD = 4
+VECTOR_PIECES = (2, 3)
+
+
+def tile_grouped_unembedding_gradient_k7_kernel(
+    tc, x, a_words, a_scales, bias, token_weight, err, running, rate, out_0, out_1, out_2
+):
+    nc = tc.nc
+    with ExitStack() as ctx:
+        keep = ctx.enter_context(tc.tile_pool(name="keep", bufs=1))
+        work = ctx.enter_context(tc.tile_pool(name="work", bufs=2))
+        psum = ctx.enter_context(tc.psum_pool(name="psum", bufs=2))
+        ctx.enter_context(tc.manual_schedule())
+
+        ident = keep.tile([P, P], F32, name="ident")
+        bias_rows = keep.tile([P, P], F32, name="bias_rows")
+        bias_raw = keep.tile([UNITS, P], BF16, name="bias_raw")
+        bias_cols = keep.tile([P, UNITS], F32, name="bias_cols")
+        a_sc = keep.tile([P, 2 * G, D], U8, name="a_sc", align_bytes=64)
+        y_sc = keep.tile([P, 2, G * D], U8, name="y_sc", align_bytes=64)
+        x_codes = keep.tile([P, 2, T], U32, name="x_codes", align_bytes=64)
+        x_sc = keep.tile([P, 2, T], U8, name="x_sc", align_bytes=64)
+
+        x_raw, x_int, a_w, tw, rt, run, e_raw, e_int, e_codes, e_sc = {}, {}, {}, {}, {}, {}, {}, {}, {}, {}
+        s1, h_t, h_tr, h_int, h_codes, h_sc = {}, {}, {}, {}, {}, {}
+        s2, t_sum, y, y_bf, y_tr, y_int, y_codes = {}, {}, {}, {}, {}, {}, {}
+
+        def load_x(j):
+            x_raw[j] = work.tile([P, K], BF16, name="x_raw", bufs=8)
+            nc.sync.dma_start(out=x_raw[j][:], in_=x[P * j : P * (j + 1), :])
+
+        def load_stage1(h):
+            a_w[h] = work.tile([P, 2, 2 * D], U8, name="a_w", bufs=4, align_bytes=64)
+            nc.sync.dma_start(
+                out=a_w[h][:].bitcast(I32),
+                in_=a_words[2 * h : 2 * h + 2].rearrange("g p n -> p g n").bitcast(I32),
+            )
+            tw[h] = work.tile([P, T], BF16, name="tw", bufs=4)
+            nc.sync.dma_start(out=tw[h][:], in_=token_weight[h].partition_broadcast(P))
+
+        def load_err(piece):
+            h, half, g = piece // 4, piece % 4 // 2, piece % 2
+            e_raw[piece] = work.tile([P, 4, BANK], BF16, name="e_raw", bufs=6)
+            rows = err[h, PASS * g : PASS * (g + 1), BANK * half : BANK * (half + 1)]
+            nc.sync.dma_start(out=e_raw[piece][:], in_=rows.rearrange("(p j) v -> p j v", j=4))
+
+        def load_running(n):
+            h, j = divmod(n, TILES)
+            if j == 0:
+                rt[h] = work.tile([P, V], BF16, name="rt", bufs=2)
+                nc.sync.dma_start(out=rt[h][:], in_=rate[h].partition_broadcast(P))
+            run[n] = work.tile([P, V], BF16, name="run", bufs=5)
+            nc.sync.dma_start(out=run[n][:], in_=running[h, P * j : P * (j + 1), :])
+
+        def turn_x(j):
+            half = j // 4
+            if j % 4 == 0:
+                x_int[half] = work.tile([P, 2, PASS * 4], BF16, name="x_int", bufs=2, align_bytes=64)
+            words = x_raw[j][:].bitcast(F32)
+            bank = psum.tile([P, 4, P], F32, name="tr", bufs=4)
+            for g in range(2):
+                for u in range(2):
+                    nc.tensor.transpose(bank[:, 2 * g + u, :], words[:, 256 * g + u : 256 * (g + 1) : 2], ident[:])
+            dst = x_int[half][:].bitcast(F32).rearrange("p g (m u) -> p g m u", u=2)
+            nc.scalar.copy(
+                out=dst[:, :, P * (j % 4) : P * (j % 4 + 1), :],
+                in_=bank[:].rearrange("p (g u) m -> p g m u", u=2),
+            )
+
+        def quantize_x(pair):
+            cols = slice(2 * P * pair, 2 * P * (pair + 1))
+            src = slice(8 * P * (pair % 2), 8 * P * (pair % 2 + 1))
+            for g in range(2):
+                nc.vector.quantize_mx(
+                    out=x_codes[:, g, cols].bitcast(FP8X4), scales=x_sc[:, g, cols], in_=x_int[pair // 2][:, g, src]
+                )
+
+        def interleave_err(piece):
+            e_int[piece] = work.tile([P, BANK, 4], BF16, name="e_int", bufs=3, align_bytes=64)
+            dst = e_int[piece][:].rearrange("p (c i) t -> p c t i", i=4)
+            src = e_raw[piece][:].rearrange("p t (c i) -> p c t i", i=4)
+            if piece in VECTOR_PIECES:
+                nc.vector.tensor_copy(out=dst, in_=src)
+            else:
+                nc.scalar.copy(out=dst, in_=src)
+
+        def quantize_err(piece):
+            e_codes[piece] = work.tile([P, BANK], U32, name="e_codes", bufs=8, align_bytes=64)
+            e_sc[piece] = work.tile([P, BANK], U8, name="e_sc", bufs=8, align_bytes=64)
+            nc.vector.quantize_mx(
+                out=e_codes[piece][:].bitcast(FP8X4),
+                scales=e_sc[piece][:],
+                in_=e_int[piece][:].rearrange("p c t -> p (c t)"),
+            )
+
+        def project(n, half, banks="s1"):
+            h, j = divmod(n, TILES)
+            s1[n, half] = psum.tile([P, BANK], F32, name=banks, bufs=2)
+            cols = slice(BANK * half, BANK * (half + 1))
+            for g in range(2):
+                nc.tensor.matmul_mx(
+                    out=s1[n, half][:],
+                    lhsT=a_w[h][:, g, 2 * P * j : 2 * P * (j + 1)].bitcast(FP4X4),
+                    lhsT_scale=a_sc[:, 2 * h + g, P * j : P * (j + 1)],
+                    rhs=x_codes[:, g, cols].bitcast(FP8X4),
+                    rhs_scale=x_sc[:, g, cols],
+                    start=(g == 0),
+                    stop=(g == 1),
+                )
+
+        def weigh(n, half):
+            if half == 0:
+                h_t[n] = work.tile([P, T], BF16, name="h_t", bufs=LEAD)
+            cols = slice(BANK * half, BANK * (half + 1))
+            nc.vector.scalar_tensor_tensor(
+                out=h_t[n][:, cols],
+                in0=s1[n, half][:],
+                scalar=bias_cols[:, n : n + 1],
+                in1=tw[n // TILES][:, cols],
+                op0=ADD,
+                op1=MULT,
+            )
+
+        def turn_h(n):
+            words = h_t[n][:].bitcast(F32)
+            h_tr[n] = psum.tile([P, 4, P], F32, name="tr", bufs=4)
+            for g in range(2):
+                for u in range(2):
+                    nc.tensor.transpose(
+                        h_tr[n][:, 2 * g + u, :], words[:, 256 * g + u : 256 * (g + 1) : 2], ident[:]
+                    )
+
+        def gather_h(n):
+            h_int[n] = work.tile([P, T], BF16, name="h_int", bufs=LEAD, align_bytes=64)
+            nc.scalar.copy(
+                out=h_int[n][:].bitcast(F32).rearrange("p (g d u) -> p g d u", g=2, u=2),
+                in_=h_tr[n][:].rearrange("p (g u) d -> p g d u", u=2),
+            )
+
+        def quantize_h(n):
+            h_codes[n] = work.tile([P, 2 * P], U32, name="h_codes", bufs=LEAD + 1, align_bytes=64)
+            h_sc[n] = work.tile([P, 2 * P], U8, name="h_sc", bufs=LEAD + 1, align_bytes=64)
+            nc.vector.quantize_mx(out=h_codes[n][:].bitcast(FP8X4), scales=h_sc[n][:], in_=h_int[n][:])
+
+        def gradient(n, half):
+            s2[n, half] = psum.tile([P, BANK], F32, name="s2", bufs=2)
+            for g in range(2):
+                piece = 4 * (n // TILES) + 2 * half + g
+                nc.tensor.matmul_mx(
+                    out=s2[n, half][:],
+                    lhsT=h_codes[n][:, P * g : P * (g + 1)].bitcast(FP8X4),
+                    lhsT_scale=h_sc[n][:, P * g : P * (g + 1)],
+                    rhs=e_codes[piece][:].bitcast(FP8X4),
+                    rhs_scale=e_sc[piece][:],
+                    start=(g == 0),
+                    stop=(g == 1),
+                )
+
+        def add_running(n, half):
+            if half == 0:
+                t_sum[n] = work.tile([P, V], F32, name="t_sum", bufs=2)
+            cols = slice(BANK * half, BANK * (half + 1))
+            nc.vector.scalar_tensor_tensor(
+                out=t_sum[n][:, cols], in0=run[n][:, cols], scalar=BETA, in1=s2[n, half][:], op0=MULT, op1=ADD
+            )
+
+        def scale(n, cols, engine=nc.vector):
+            h, j = divmod(n, TILES)
+            if cols.start == 0:
+                y[n] = work.tile([P, V], F32, name="y", bufs=4)
+            engine.tensor_tensor(out=y[n][:, cols], in0=t_sum[n][:, cols], in1=rt[h][:, cols], op=MULT)
+
+        def store_y(n, cols):
+            h, j = divmod(n, TILES)
+            nc.sync.dma_start(out=out_0[h, P * j : P * (j + 1), cols], in_=y[n][:, cols])
+
+        def round_y(n, groups, copy):
+            if groups.start == 0:
+                y_bf[n] = work.tile([P, V], BF16, name="y_bf", bufs=2)
+            copy(
+                out=y_bf[n][:].rearrange("p (g u m e) -> p g u m e", g=2, u=2, e=2)[:, groups],
+                in_=y[n][:].rearrange("p (g m u e) -> p g u m e", g=2, u=2, e=2)[:, groups],
+            )
+
+        def turn_y(n, groups):
+            words = y_bf[n][:].bitcast(F32)
+            y_tr[n, groups.start] = psum.tile([P, 4, P], F32, name="tr", bufs=4)
+            for q in range(2 * groups.start, 2 * groups.stop):
+                nc.tensor.transpose(y_tr[n, groups.start][:, q, :], words[:, P * q : P * (q + 1)], ident[:])
+
+        def gather_y(n, groups, copy):
+            h, j = divmod(n, TILES)
+            if j == 0 and groups.start == 0:
+                y_int[h] = work.tile([P, 2, D * 4], BF16, name="y_int", bufs=2, align_bytes=64)
+            dst = y_int[h][:].bitcast(F32).rearrange("p g (d u) -> p g d u", u=2)
+            copy(
+                out=dst[:, groups, P * j : P * (j + 1), :],
+                in_=y_tr[n, groups.start][:].rearrange("p (g u) d -> p g d u", u=2)[:, groups],
+            )
+
+        def quantize_y(h, g, cols):
+            if g == 0 and cols.start == 0:
+                y_codes[h] = work.tile([P, 2, D], U32, name="y_codes", bufs=2, align_bytes=64)
+            nc.vector.quantize_mx(
+                out=y_codes[h][:, g, cols].bitcast(FP8X4),
+                scales=y_sc[:, g, D * h + cols.start : D * h + cols.stop],
+                in_=y_int[h][:, g, 4 * cols.start : 4 * cols.stop],
+            )
+
+        def store_codes(h, cols):
+            rows = out_1.rearrange("g p m t -> p g (m t)")
+            nc.sync.dma_start(
+                out=rows[:, :, 4 * (D * h + cols.start) : 4 * (D * h + cols.stop)].bitcast(I32),
+                in_=y_codes[h][:, :, cols].bitcast(I32),
+            )
+
+        def store_scales(cols):
+            for q in range(4):
+                nc.sync.dma_start(
+                    out=out_2[:, 4 * q : 4 * q + 4, cols].rearrange("g r m -> r g m").bitcast(I32),
+                    in_=y_sc[32 * q : 32 * q + 4, :, cols].bitcast(I32),
+                )
+
+        both, whole = slice(0, 2), slice(0, V)
+        halves = [slice(0, BANK), slice(BANK, V)]
+        nc.vector.memset(a_sc[:].bitcast(I32), 0)
+        nc.vector.memset(bias_rows[:], 0.0)
+        make_identity(nc, ident[:])
+        nc.sync.dma_start(out=bias_raw[:], in_=bias.rearrange("h (j p) -> (h j) p", p=P))
+        for j in range(4):
+            load_x(j)
+        for q in range(4):
+            nc.sync.dma_start(
+                out=a_sc[32 * q : 32 * q + 4, :, :].bitcast(I32),
+                in_=a_scales[:, 4 * q : 4 * q + 4, :].rearrange("g r n -> r g n").bitcast(I32),
+            )
+        load_stage1(0)
+        load_err(0)
+        load_err(2)
+        for j in range(4, 8):
+            load_x(j)
+        load_err(1)
+        load_err(3)
+        load_running(0)
+        load_stage1(1)
+        load_err(4)
+        load_running(1)
+        load_err(5)
+        load_running(2)
+
+        nc.vector.tensor_copy(out=bias_rows[:UNITS, :], in_=bias_raw[:])
+        bias_bank = psum.tile([P, 4, P], F32, name="tr", bufs=4)
+        nc.tensor.transpose(bias_bank[:, 0, :], bias_rows[:], ident[:])
+        nc.vector.tensor_copy(out=bias_cols[:], in_=bias_bank[:, 0, :UNITS])
+        for pair in range(2):
+            turn_x(2 * pair)
+            turn_x(2 * pair + 1)
+            quantize_x(pair)
+        interleave_err(0)
+        for n in range(LEAD):
+            project(n, 0, ("s1", "s2")[n % 2])
+        for n in range(LEAD):
+            weigh(n, 0)
+        interleave_err(2)
+        quantize_err(0)
+        load_err(6)
+        turn_x(4)
+        turn_x(5)
+        quantize_x(2)
+        quantize_err(2)
+        turn_x(6)
+        turn_x(7)
+        quantize_x(3)
+        interleave_err(1)
+        for n in range(LEAD):
+            project(n, 1, ("s1", "s2")[n % 2])
+        interleave_err(3)
+        for n in range(LEAD):
+            weigh(n, 1)
+            turn_h(n)
+            gather_h(n)
+            if n == 1:
+                quantize_err(1)
+        quantize_h(0)
+        gradient(0, 0)
+        quantize_err(3)
+        gradient(0, 1)
+        project(LEAD, 0)
+        project(LEAD, 1)
+        quantize_h(1)
+        quantize_h(2)
+
+        last = UNITS - 1
+        first, second = slice(0, 1), slice(1, 2)
+
+        def finish_head(h):
+            quantize_y(h, 0, slice(0, D))
+            quantize_y(h, 1, slice(0, D))
+            store_codes(h, slice(0, D))
+
+        for s in range(UNITS - LEAD):
+            ahead = s + LEAD
+            if s + 7 < 4 * G:
+                load_err(s + 7)
+            load_running(s + 3)
+            if s in (1, 5):
+                load_stage1(s // TILES + 2)
+            interleave_err(ahead)
+            add_running(s, 0)
+            if s >= 1:
+                round_y(s - 1, both, nc.scalar.copy)
+            add_running(s, 1)
+            gradient(s + 1, 0)
+            weigh(ahead, 0)
+            weigh(ahead, 1)
+            turn_h(ahead)
+            if s >= 2:
+                turn_y(s - 2, both)
+            gather_h(ahead)
+            if s >= 2:
+                gather_y(s - 2, both, nc.scalar.copy)
+            scale(s, whole)
+            store_y(s, whole)
+            quantize_err(ahead)
+            gradient(s + 1, 1)
+            quantize_h(ahead - 1)
+            if ahead < last:
+                project(ahead + 1, 0)
+                project(ahead + 1, 1)
+            if s in (6, 10):
+                finish_head((s - 3) // TILES)
+
+        s = UNITS - LEAD
+        load_running(last)
+        turn_y(s - 2, both)
+        round_y(s - 1, both, nc.scalar.copy)
+        gather_y(s - 2, both, nc.scalar.copy)
+        for s in range(UNITS - LEAD, UNITS):
+            add_running(s, 0)
+            if s < last:
+                gradient(s + 1, 0)
+            if s == UNITS - LEAD:
+                quantize_h(last)
+                turn_y(s - 1, both)
+                gather_y(s - 1, both, nc.scalar.copy)
+            else:
+                scale(s - 1, halves[1])
+                store_y(s - 1, whole)
+                turn_y(s - 1, first)
+                round_y(s - 1, second, nc.scalar.copy)
+                gather_y(s - 1, first, nc.scalar.copy)
+            add_running(s, 1)
+            if s < last:
+                gradient(s + 1, 1)
+            scale(s, halves[0])
+            if s > UNITS - LEAD:
+                turn_y(s - 1, second)
+            round_y(s, first, nc.scalar.copy)
+            if s > UNITS - LEAD:
+                gather_y(s - 1, second, nc.scalar.copy)
+            if s == UNITS - LEAD + 1:
+                finish_head(G - 2)
+                store_scales(slice(0, D * (G - 1)))
+        h = G - 1
+        store_y(last, halves[0])
+        quantize_y(h, 0, slice(0, 2 * P))
+        scale(last, halves[1])
+        store_y(last, halves[1])
+        turn_y(last, first)
+        quantize_y(h, 1, slice(0, 2 * P))
+        round_y(last, second, nc.vector.tensor_copy)
+        turn_y(last, second)
+        gather_y(last, first, nc.scalar.copy)
+        gather_y(last, second, nc.scalar.copy)
+        quantize_y(h, 0, slice(2 * P, 3 * P))
+        quantize_y(h, 1, slice(2 * P, 3 * P))
+        store_codes(h, slice(0, 3 * P))
+        quantize_y(h, 0, slice(3 * P, 4 * P))
+        quantize_y(h, 1, slice(3 * P, 4 * P))
+        store_codes(h, slice(3 * P, 4 * P))
+        store_scales(slice(D * (G - 1), G * D))

@@ -23,7 +23,8 @@ BANK = 512
 TILES = D // P
 UNITS = G * TILES
 LEAD = 4
-VECTOR_PIECES = (2, 3)
+GPSIMD_COLS = 832
+VECTOR_PIECES = (2,)
 
 
 def tile_grouped_unembedding_gradient_k7_kernel(
@@ -46,6 +47,7 @@ def tile_grouped_unembedding_gradient_k7_kernel(
         x_sc = keep.tile([P, 2, T], U8, name="x_sc", align_bytes=64)
 
         x_raw, x_int, a_w, tw, rt, run, e_raw, e_int, e_codes, e_sc = {}, {}, {}, {}, {}, {}, {}, {}, {}, {}
+        x_srt = {}
         s1, h_t, h_tr, h_int, h_codes, h_sc = {}, {}, {}, {}, {}, {}
         s2, t_sum, y, y_bf, y_tr, y_int, y_codes = {}, {}, {}, {}, {}, {}, {}
 
@@ -76,15 +78,20 @@ def tile_grouped_unembedding_gradient_k7_kernel(
             run[n] = work.tile([P, V], BF16, name="run", bufs=5)
             nc.sync.dma_start(out=run[n][:], in_=running[h, P * j : P * (j + 1), :])
 
+        def sort_x(j):
+            x_srt[j] = work.tile([P, 4, P], F32, name="x_srt", bufs=3)
+            nc.vector.tensor_copy(
+                out=x_srt[j][:].rearrange("p (g u) m -> p g u m", u=2),
+                in_=x_raw[j][:].bitcast(F32).rearrange("p (g m u) -> p g u m", g=2, u=2),
+            )
+
         def turn_x(j):
             half = j // 4
             if j % 4 == 0:
                 x_int[half] = work.tile([P, 2, PASS * 4], BF16, name="x_int", bufs=2, align_bytes=64)
-            words = x_raw[j][:].bitcast(F32)
             bank = psum.tile([P, 4, P], F32, name="tr", bufs=4)
-            for g in range(2):
-                for u in range(2):
-                    nc.tensor.transpose(bank[:, 2 * g + u, :], words[:, 256 * g + u : 256 * (g + 1) : 2], ident[:])
+            for q in range(4):
+                nc.tensor.transpose(bank[:, q, :], x_srt[j][:, q, :], ident[:])
             dst = x_int[half][:].bitcast(F32).rearrange("p g (m u) -> p g m u", u=2)
             nc.scalar.copy(
                 out=dst[:, :, P * (j % 4) : P * (j % 4 + 1), :],
@@ -100,7 +107,7 @@ def tile_grouped_unembedding_gradient_k7_kernel(
                 )
 
         def interleave_err(piece):
-            e_int[piece] = work.tile([P, BANK, 4], BF16, name="e_int", bufs=3, align_bytes=64)
+            e_int[piece] = work.tile([P, BANK, 4], BF16, name="e_int", bufs=4, align_bytes=64)
             dst = e_int[piece][:].rearrange("p (c i) t -> p c t i", i=4)
             src = e_raw[piece][:].rearrange("p t (c i) -> p c t i", i=4)
             if piece in VECTOR_PIECES:
@@ -251,20 +258,17 @@ def tile_grouped_unembedding_gradient_k7_kernel(
         nc.vector.memset(bias_rows[:], 0.0)
         make_identity(nc, ident[:])
         nc.sync.dma_start(out=bias_raw[:], in_=bias.rearrange("h (j p) -> (h j) p", p=P))
-        for j in range(4):
+        for j in range(8):
             load_x(j)
-        for q in range(4):
-            nc.sync.dma_start(
-                out=a_sc[32 * q : 32 * q + 4, :, :].bitcast(I32),
-                in_=a_scales[:, 4 * q : 4 * q + 4, :].rearrange("g r n -> r g n").bitcast(I32),
-            )
+            if j == 7:
+                for q in range(4):
+                    nc.sync.dma_start(
+                        out=a_sc[32 * q : 32 * q + 4, :, :].bitcast(I32),
+                        in_=a_scales[:, 4 * q : 4 * q + 4, :].rearrange("g r n -> r g n").bitcast(I32),
+                    )
         load_stage1(0)
-        load_err(0)
-        load_err(2)
-        for j in range(4, 8):
-            load_x(j)
-        load_err(1)
-        load_err(3)
+        for piece in range(4):
+            load_err(piece)
         load_running(0)
         load_stage1(1)
         load_err(4)
@@ -275,43 +279,51 @@ def tile_grouped_unembedding_gradient_k7_kernel(
         nc.vector.tensor_copy(out=bias_rows[:UNITS, :], in_=bias_raw[:])
         bias_bank = psum.tile([P, 4, P], F32, name="tr", bufs=4)
         nc.tensor.transpose(bias_bank[:, 0, :], bias_rows[:], ident[:])
-        nc.vector.tensor_copy(out=bias_cols[:], in_=bias_bank[:, 0, :UNITS])
-        for pair in range(2):
-            turn_x(2 * pair)
-            turn_x(2 * pair + 1)
-            quantize_x(pair)
-        interleave_err(0)
-        for n in range(LEAD):
-            project(n, 0, ("s1", "s2")[n % 2])
-        for n in range(LEAD):
-            weigh(n, 0)
-        interleave_err(2)
-        quantize_err(0)
-        load_err(6)
-        turn_x(4)
-        turn_x(5)
-        quantize_x(2)
-        quantize_err(2)
-        turn_x(6)
-        turn_x(7)
+        for j in range(8):
+            sort_x(j)
+            turn_x(j)
+            if j == 0:
+                nc.vector.tensor_copy(out=bias_cols[:], in_=bias_bank[:, 0, :UNITS])
+            if j in (4, 6, 7):
+                quantize_x((4, 6, 7).index(j))
         quantize_x(3)
+        interleave_err(0)
         interleave_err(1)
-        for n in range(LEAD):
-            project(n, 1, ("s1", "s2")[n % 2])
-        interleave_err(3)
-        for n in range(LEAD):
+        load_err(6)
+        project(0, 0, "s1")
+        project(1, 0, "s2")
+        project(0, 1, "s1")
+        project(1, 1, "s2")
+        for n in range(2):
+            weigh(n, 0)
+            project(n + 2, 0, ("s1", "s2")[n])
+        for n in range(2):
             weigh(n, 1)
-            turn_h(n)
-            gather_h(n)
-            if n == 1:
-                quantize_err(1)
+            project(n + 2, 1, ("s1", "s2")[n])
+        turn_h(0)
+        turn_h(1)
+        gather_h(0)
+        gather_h(1)
+        quantize_err(0)
+        weigh(2, 0)
+        weigh(3, 0)
+        project(LEAD, 0)
+        weigh(2, 1)
+        weigh(3, 1)
+        turn_h(2)
+        project(LEAD, 1)
+        turn_h(3)
+        interleave_err(3)
+        quantize_err(1)
         quantize_h(0)
         gradient(0, 0)
+        interleave_err(2)
+        gather_h(2)
+        gather_h(3)
+        quantize_h(1)
+        quantize_err(2)
         quantize_err(3)
         gradient(0, 1)
-        project(LEAD, 0)
-        project(LEAD, 1)
-        quantize_h(1)
         quantize_h(2)
 
         last = UNITS - 1
@@ -331,26 +343,30 @@ def tile_grouped_unembedding_gradient_k7_kernel(
                 load_stage1(s // TILES + 2)
             interleave_err(ahead)
             add_running(s, 0)
+            scale(s, halves[0], nc.gpsimd)
+            gradient(s + 1, 0)
             if s >= 1:
                 round_y(s - 1, both, nc.scalar.copy)
             add_running(s, 1)
-            gradient(s + 1, 0)
-            weigh(ahead, 0)
-            weigh(ahead, 1)
-            turn_h(ahead)
+            split = GPSIMD_COLS if s >= 2 else GPSIMD_COLS - 2 * P
+            scale(s, slice(BANK, split), nc.gpsimd)
             if s >= 2:
                 turn_y(s - 2, both)
+            weigh(ahead, 0)
+            if ahead < last:
+                project(ahead + 1, 0)
+            weigh(ahead, 1)
+            turn_h(ahead)
+            if ahead < last:
+                project(ahead + 1, 1)
             gather_h(ahead)
             if s >= 2:
-                gather_y(s - 2, both, nc.scalar.copy)
-            scale(s, whole)
+                gather_y(s - 2, both, nc.vector.tensor_copy)
+            scale(s, slice(split, V))
             store_y(s, whole)
             quantize_err(ahead)
             gradient(s + 1, 1)
             quantize_h(ahead - 1)
-            if ahead < last:
-                project(ahead + 1, 0)
-                project(ahead + 1, 1)
             if s in (6, 10):
                 finish_head((s - 3) // TILES)
 

@@ -23,6 +23,7 @@ BANK = 512
 TILES = D // P
 UNITS = G * TILES
 LEAD = 4
+RATE_ROW = 32
 GPSIMD_COLS = 832
 VECTOR_PIECES = (2,)
 
@@ -40,6 +41,8 @@ def tile_grouped_unembedding_gradient_k7_kernel(
         ident = keep.tile([P, P], F32, name="ident")
         bias_rows = keep.tile([P, P], F32, name="bias_rows")
         bias_raw = keep.tile([UNITS, P], BF16, name="bias_raw")
+        vec_rows = keep.tile([P, P], F32, name="vec_rows")
+        vec_cols = keep.tile([P, RATE_ROW + 4 * G], F32, name="vec_cols")
         bias_cols = keep.tile([P, UNITS], F32, name="bias_cols")
         a_sc = keep.tile([P, 2 * G, D], U8, name="a_sc", align_bytes=64)
         y_sc = keep.tile([P, 2, G * D], U8, name="y_sc", align_bytes=64)
@@ -47,7 +50,7 @@ def tile_grouped_unembedding_gradient_k7_kernel(
         x_sc = keep.tile([P, 2, T], U8, name="x_sc", align_bytes=64)
 
         x_raw, x_int, a_w, tw, rt, run, e_raw, e_int, e_codes, e_sc = {}, {}, {}, {}, {}, {}, {}, {}, {}, {}
-        x_srt = {}
+        x_srt, spread_bank = {}, {}
         s1, h_t, h_tr, h_int, h_codes, h_sc = {}, {}, {}, {}, {}, {}
         s2, t_sum, y, y_bf, y_tr, y_int, y_codes = {}, {}, {}, {}, {}, {}, {}
 
@@ -61,22 +64,37 @@ def tile_grouped_unembedding_gradient_k7_kernel(
                 out=a_w[h][:].bitcast(I32),
                 in_=a_words[2 * h : 2 * h + 2].rearrange("g p n -> p g n").bitcast(I32),
             )
-            tw[h] = work.tile([P, T], BF16, name="tw", bufs=4)
-            nc.sync.dma_start(out=tw[h][:], in_=token_weight[h].partition_broadcast(P))
 
-        def load_err(piece):
-            h, half, g = piece // 4, piece % 4 // 2, piece % 2
-            e_raw[piece] = work.tile([P, 4, BANK], BF16, name="e_raw", bufs=6)
-            rows = err[h, PASS * g : PASS * (g + 1), BANK * half : BANK * (half + 1)]
-            nc.sync.dma_start(out=e_raw[piece][:], in_=rows.rearrange("(p j) v -> p j v", j=4))
+        def load_err(h, g, cols):
+            raw = work.tile([P, 4, cols.stop - cols.start], BF16, name="e_raw", bufs=4)
+            rows = err[h, PASS * g : PASS * (g + 1), cols]
+            nc.sync.dma_start(out=raw[:], in_=rows.rearrange("(p j) v -> p j v", j=4))
+            for first in range(cols.start, cols.stop, BANK):
+                offset = first - cols.start
+                e_raw[4 * h + 2 * (first // BANK) + g] = raw[:, :, offset : offset + BANK]
 
         def load_running(n):
             h, j = divmod(n, TILES)
-            if j == 0:
-                rt[h] = work.tile([P, V], BF16, name="rt", bufs=2)
-                nc.sync.dma_start(out=rt[h][:], in_=rate[h].partition_broadcast(P))
             run[n] = work.tile([P, V], BF16, name="run", bufs=5)
             nc.sync.dma_start(out=run[n][:], in_=running[h, P * j : P * (j + 1), :])
+
+        def spread(first_row, banks="tr", bufs=4):
+            spread_bank[first_row] = psum.tile([P, 4, P], F32, name=banks, bufs=bufs)
+            for q in range(4):
+                column = vec_cols[:, first_row + q : first_row + q + 1]
+                nc.tensor.transpose(spread_bank[first_row][:, q, :], column.to_broadcast([P, P]), ident[:])
+
+        def gather_weight(h, copy):
+            tw[h] = work.tile([P, T], BF16, name="tw", bufs=G)
+            words = spread_bank[4 * h][:].rearrange("p q w -> p (q w)")
+            copy(
+                out=tw[h][:].bitcast(F32).rearrange("p (g u m) -> p g u m", g=2, u=2),
+                in_=words.rearrange("p (g m u) -> p g u m", g=2, u=2),
+            )
+
+        def gather_rate(h, copy):
+            rt[h] = work.tile([P, V], BF16, name="rt", bufs=G)
+            copy(out=rt[h][:].bitcast(F32), in_=spread_bank[RATE_ROW + 4 * h][:].rearrange("p q w -> p (q w)"))
 
         def sort_x(j):
             x_srt[j] = work.tile([P, 4, P], F32, name="x_srt", bufs=3)
@@ -92,24 +110,21 @@ def tile_grouped_unembedding_gradient_k7_kernel(
             bank = psum.tile([P, 4, P], F32, name="tr", bufs=4)
             for q in range(4):
                 nc.tensor.transpose(bank[:, q, :], x_srt[j][:, q, :], ident[:])
-            dst = x_int[half][:].bitcast(F32).rearrange("p g (m u) -> p g m u", u=2)
-            nc.scalar.copy(
-                out=dst[:, :, P * (j % 4) : P * (j % 4 + 1), :],
-                in_=bank[:].rearrange("p (g u) m -> p g m u", u=2),
+            dst = x_int[half][:].bitcast(F32).rearrange("p g (u j m e w) -> p g j u m e w", u=2, j=4, e=2, w=2)
+            src = bank[:].rearrange("p (g w) (m u e) -> p g u m e w", w=2, u=2, e=2)
+            for g in range(2):
+                nc.scalar.copy(out=dst[:, g, j % 4], in_=src[:, g])
+
+        def quantize_x(half, g):
+            cols = slice(PASS * half, PASS * (half + 1))
+            nc.vector.quantize_mx(
+                out=x_codes[:, g, cols].bitcast(FP8X4), scales=x_sc[:, g, cols], in_=x_int[half][:, g, :]
             )
 
-        def quantize_x(pair):
-            cols = slice(2 * P * pair, 2 * P * (pair + 1))
-            src = slice(8 * P * (pair % 2), 8 * P * (pair % 2 + 1))
-            for g in range(2):
-                nc.vector.quantize_mx(
-                    out=x_codes[:, g, cols].bitcast(FP8X4), scales=x_sc[:, g, cols], in_=x_int[pair // 2][:, g, src]
-                )
-
         def interleave_err(piece):
-            e_int[piece] = work.tile([P, BANK, 4], BF16, name="e_int", bufs=4, align_bytes=64)
+            e_int[piece] = work.tile([P, BANK, 4], BF16, name="e_int", bufs=3, align_bytes=64)
             dst = e_int[piece][:].rearrange("p (c i) t -> p c t i", i=4)
-            src = e_raw[piece][:].rearrange("p t (c i) -> p c t i", i=4)
+            src = e_raw[piece].rearrange("p t (c i) -> p c t i", i=4)
             if piece in VECTOR_PIECES:
                 nc.vector.tensor_copy(out=dst, in_=src)
             else:
@@ -155,11 +170,8 @@ def tile_grouped_unembedding_gradient_k7_kernel(
         def turn_h(n):
             words = h_t[n][:].bitcast(F32)
             h_tr[n] = psum.tile([P, 4, P], F32, name="tr", bufs=4)
-            for g in range(2):
-                for u in range(2):
-                    nc.tensor.transpose(
-                        h_tr[n][:, 2 * g + u, :], words[:, 256 * g + u : 256 * (g + 1) : 2], ident[:]
-                    )
+            for q in range(4):
+                nc.tensor.transpose(h_tr[n][:, q, :], words[:, P * q : P * (q + 1)], ident[:])
 
         def gather_h(n):
             h_int[n] = work.tile([P, T], BF16, name="h_int", bufs=LEAD, align_bytes=64)
@@ -254,42 +266,55 @@ def tile_grouped_unembedding_gradient_k7_kernel(
 
         both, whole = slice(0, 2), slice(0, V)
         halves = [slice(0, BANK), slice(BANK, V)]
-        nc.vector.memset(a_sc[:].bitcast(I32), 0)
+        nc.vector.memset(vec_rows[:], 0.0)
         nc.vector.memset(bias_rows[:], 0.0)
+        nc.vector.memset(a_sc[:].bitcast(I32), 0)
         make_identity(nc, ident[:])
+        for first_row, vec in ((0, token_weight), (RATE_ROW, rate)):
+            nc.sync.dma_start(
+                out=vec_rows[first_row : first_row + 4 * G, :].bitcast(BF16),
+                in_=vec.rearrange("h (q w) -> (h q) w", q=4),
+            )
         nc.sync.dma_start(out=bias_raw[:], in_=bias.rearrange("h (j p) -> (h j) p", p=P))
         for j in range(8):
             load_x(j)
-            if j == 7:
-                for q in range(4):
-                    nc.sync.dma_start(
-                        out=a_sc[32 * q : 32 * q + 4, :, :].bitcast(I32),
-                        in_=a_scales[:, 4 * q : 4 * q + 4, :].rearrange("g r n -> r g n").bitcast(I32),
-                    )
-        load_stage1(0)
-        for piece in range(4):
-            load_err(piece)
-        load_running(0)
-        load_stage1(1)
-        load_err(4)
-        load_running(1)
-        load_err(5)
-        load_running(2)
 
+        vec_bank = psum.tile([P, 4, P], F32, name="tr", bufs=4)
+        nc.tensor.transpose(vec_bank[:, 0, :], vec_rows[:], ident[:])
+        nc.vector.tensor_copy(out=vec_cols[:], in_=vec_bank[:, 0, : RATE_ROW + 4 * G])
         nc.vector.tensor_copy(out=bias_rows[:UNITS, :], in_=bias_raw[:])
-        bias_bank = psum.tile([P, 4, P], F32, name="tr", bufs=4)
-        nc.tensor.transpose(bias_bank[:, 0, :], bias_rows[:], ident[:])
         for j in range(8):
             sort_x(j)
             turn_x(j)
             if j == 0:
+                bias_bank = psum.tile([P, 4, P], F32, name="tr", bufs=4)
+                nc.tensor.transpose(bias_bank[:, 0, :], bias_rows[:], ident[:])
+            if j == 5:
+                spread(0, "s2", 2)
+            if j == 1:
                 nc.vector.tensor_copy(out=bias_cols[:], in_=bias_bank[:, 0, :UNITS])
-            if j in (4, 6, 7):
-                quantize_x((4, 6, 7).index(j))
-        quantize_x(3)
+        quantize_x(0, 0)
+        quantize_x(0, 1)
+        gather_weight(0, nc.vector.tensor_copy)
+        for q in range(4):
+            nc.sync.dma_start(
+                out=a_sc[32 * q : 32 * q + 4, :, :].bitcast(I32),
+                in_=a_scales[:, 4 * q : 4 * q + 4, :].rearrange("g r n -> r g n").bitcast(I32),
+            )
+        load_stage1(0)
+        for half in range(2):
+            for g in range(2):
+                load_err(0, g, halves[half])
+        load_running(0)
+        load_stage1(1)
+        load_running(1)
+        quantize_x(1, 0)
+        quantize_x(1, 1)
         interleave_err(0)
+        load_err(1, 0, whole)
+        load_running(2)
         interleave_err(1)
-        load_err(6)
+        load_err(1, 1, whole)
         project(0, 0, "s1")
         project(1, 0, "s2")
         project(0, 1, "s1")
@@ -300,31 +325,32 @@ def tile_grouped_unembedding_gradient_k7_kernel(
         for n in range(2):
             weigh(n, 1)
             project(n + 2, 1, ("s1", "s2")[n])
-        turn_h(0)
-        turn_h(1)
-        gather_h(0)
-        gather_h(1)
+            turn_h(n)
+            gather_h(n)
         quantize_err(0)
+        spread(RATE_ROW)
+        spread(4)
+        interleave_err(3)
+        gather_rate(0, nc.scalar.copy)
+        gather_weight(1, nc.scalar.copy)
         weigh(2, 0)
         weigh(3, 0)
         project(LEAD, 0)
         weigh(2, 1)
         weigh(3, 1)
-        turn_h(2)
-        project(LEAD, 1)
-        turn_h(3)
-        interleave_err(3)
         quantize_err(1)
         quantize_h(0)
         gradient(0, 0)
+        project(LEAD, 1)
         interleave_err(2)
+        turn_h(2)
+        turn_h(3)
         gather_h(2)
         gather_h(3)
         quantize_h(1)
         quantize_err(2)
         quantize_err(3)
         gradient(0, 1)
-        quantize_h(2)
 
         last = UNITS - 1
         first, second = slice(0, 1), slice(1, 2)
@@ -336,8 +362,8 @@ def tile_grouped_unembedding_gradient_k7_kernel(
 
         for s in range(UNITS - LEAD):
             ahead = s + LEAD
-            if s + 7 < 4 * G:
-                load_err(s + 7)
+            if s in (0, 1, 4, 5):
+                load_err(s // TILES + 2, s % 2, whole)
             load_running(s + 3)
             if s in (1, 5):
                 load_stage1(s // TILES + 2)
@@ -348,10 +374,13 @@ def tile_grouped_unembedding_gradient_k7_kernel(
             if s >= 1:
                 round_y(s - 1, both, nc.scalar.copy)
             add_running(s, 1)
-            split = GPSIMD_COLS if s >= 2 else GPSIMD_COLS - 2 * P
-            scale(s, slice(BANK, split), nc.gpsimd)
+            scale(s, slice(BANK, GPSIMD_COLS), nc.gpsimd)
             if s >= 2:
                 turn_y(s - 2, both)
+            else:
+                spread(4 * (s + 2))
+                spread(RATE_ROW + 4 * (s + 1))
+                gather_rate(s + 1, nc.scalar.copy)
             weigh(ahead, 0)
             if ahead < last:
                 project(ahead + 1, 0)
@@ -362,18 +391,24 @@ def tile_grouped_unembedding_gradient_k7_kernel(
             gather_h(ahead)
             if s >= 2:
                 gather_y(s - 2, both, nc.vector.tensor_copy)
-            scale(s, slice(split, V))
+            else:
+                gather_weight(s + 2, nc.vector.tensor_copy)
+            scale(s, slice(GPSIMD_COLS, V))
             store_y(s, whole)
             quantize_err(ahead)
             gradient(s + 1, 1)
+            if s == 0:
+                quantize_h(2)
             quantize_h(ahead - 1)
             if s in (6, 10):
                 finish_head((s - 3) // TILES)
 
         s = UNITS - LEAD
         load_running(last)
-        turn_y(s - 2, both)
         round_y(s - 1, both, nc.scalar.copy)
+        spread(RATE_ROW + 4 * (G - 1))
+        turn_y(s - 2, both)
+        gather_rate(G - 1, nc.scalar.copy)
         gather_y(s - 2, both, nc.scalar.copy)
         for s in range(UNITS - LEAD, UNITS):
             add_running(s, 0)

@@ -24,8 +24,8 @@ TILES = D // P
 UNITS = G * TILES
 LEAD = 4
 RATE_ROW = 32
-GPSIMD_COLS = 832
-VECTOR_PIECES = (2,)
+GPSIMD_HALVES = 3
+SCALAR_ROUNDS = 6
 
 
 def tile_grouped_unembedding_gradient_k7_kernel(
@@ -55,11 +55,11 @@ def tile_grouped_unembedding_gradient_k7_kernel(
         s2, t_sum, y, y_bf, y_tr, y_int, y_codes = {}, {}, {}, {}, {}, {}, {}
 
         def load_x(j):
-            x_raw[j] = work.tile([P, K], BF16, name="x_raw", bufs=8)
+            x_raw[j] = work.tile([P, K], BF16, name="x_raw", bufs=7)
             nc.sync.dma_start(out=x_raw[j][:], in_=x[P * j : P * (j + 1), :])
 
         def load_stage1(h):
-            a_w[h] = work.tile([P, 2, 2 * D], U8, name="a_w", bufs=4, align_bytes=64)
+            a_w[h] = work.tile([P, 2, 2 * D], U8, name="a_w", bufs=2, align_bytes=64)
             nc.sync.dma_start(
                 out=a_w[h][:].bitcast(I32),
                 in_=a_words[2 * h : 2 * h + 2].rearrange("g p n -> p g n").bitcast(I32),
@@ -106,7 +106,7 @@ def tile_grouped_unembedding_gradient_k7_kernel(
         def turn_x(j):
             half = j // 4
             if j % 4 == 0:
-                x_int[half] = work.tile([P, 2, PASS * 4], BF16, name="x_int", bufs=2, align_bytes=64)
+                x_int[half] = work.tile([P, 2, PASS * 4], BF16, name="staged", bufs=3, align_bytes=64)
             bank = psum.tile([P, 4, P], F32, name="tr", bufs=4)
             for q in range(4):
                 nc.tensor.transpose(bank[:, q, :], x_srt[j][:, q, :], ident[:])
@@ -121,22 +121,23 @@ def tile_grouped_unembedding_gradient_k7_kernel(
                 out=x_codes[:, g, cols].bitcast(FP8X4), scales=x_sc[:, g, cols], in_=x_int[half][:, g, :]
             )
 
-        def interleave_err(piece):
-            e_int[piece] = work.tile([P, BANK, 4], BF16, name="e_int", bufs=3, align_bytes=64)
-            dst = e_int[piece][:].rearrange("p (c i) t -> p c t i", i=4)
-            src = e_raw[piece].rearrange("p t (c i) -> p c t i", i=4)
-            if piece in VECTOR_PIECES:
-                nc.vector.tensor_copy(out=dst, in_=src)
-            else:
-                nc.scalar.copy(out=dst, in_=src)
+        def interleave_err(piece, copy):
+            pair, g = divmod(piece, 2)
+            if pair not in e_int:
+                e_int[pair] = work.tile([P, 2, BANK * 4], BF16, name="staged", bufs=3, align_bytes=64)
+            copy(
+                out=e_int[pair][:, g, :].rearrange("p (c i t) -> p c t i", i=4, t=4),
+                in_=e_raw[piece].rearrange("p t (c i) -> p c t i", i=4),
+            )
 
-        def quantize_err(piece):
-            e_codes[piece] = work.tile([P, BANK], U32, name="e_codes", bufs=8, align_bytes=64)
-            e_sc[piece] = work.tile([P, BANK], U8, name="e_sc", bufs=8, align_bytes=64)
+        def quantize_err(pair, groups):
+            if groups.start == 0:
+                e_codes[pair] = work.tile([P, 2, BANK], U32, name="e_codes", bufs=4, align_bytes=64)
+                e_sc[pair] = work.tile([P, 2, BANK], U8, name="e_sc", bufs=4, align_bytes=64)
             nc.vector.quantize_mx(
-                out=e_codes[piece][:].bitcast(FP8X4),
-                scales=e_sc[piece][:],
-                in_=e_int[piece][:].rearrange("p c t -> p (c t)"),
+                out=e_codes[pair][:, groups, :].rearrange("p g c -> p (g c)").bitcast(FP8X4),
+                scales=e_sc[pair][:, groups, :].rearrange("p g c -> p (g c)"),
+                in_=e_int[pair][:, groups, :].rearrange("p g c -> p (g c)"),
             )
 
         def project(n, half, banks="s1"):
@@ -174,34 +175,40 @@ def tile_grouped_unembedding_gradient_k7_kernel(
                 nc.tensor.transpose(h_tr[n][:, q, :], words[:, P * q : P * (q + 1)], ident[:])
 
         def gather_h(n):
-            h_int[n] = work.tile([P, T], BF16, name="h_int", bufs=LEAD, align_bytes=64)
+            if n % 2 == 0:
+                h_int[n // 2] = work.tile([P, 2, T], BF16, name="h_int", bufs=2, align_bytes=64)
             nc.scalar.copy(
-                out=h_int[n][:].bitcast(F32).rearrange("p (g d u) -> p g d u", g=2, u=2),
+                out=h_int[n // 2][:, n % 2, :].bitcast(F32).rearrange("p (g d u) -> p g d u", g=2, u=2),
                 in_=h_tr[n][:].rearrange("p (g u) d -> p g d u", u=2),
             )
 
-        def quantize_h(n):
-            h_codes[n] = work.tile([P, 2 * P], U32, name="h_codes", bufs=LEAD + 1, align_bytes=64)
-            h_sc[n] = work.tile([P, 2 * P], U8, name="h_sc", bufs=LEAD + 1, align_bytes=64)
-            nc.vector.quantize_mx(out=h_codes[n][:].bitcast(FP8X4), scales=h_sc[n][:], in_=h_int[n][:])
+        def quantize_h(pair, tiles):
+            if tiles.start == 0:
+                h_codes[pair] = work.tile([P, 2, 2 * P], U32, name="h_codes", bufs=3, align_bytes=64)
+                h_sc[pair] = work.tile([P, 2, 2 * P], U8, name="h_sc", bufs=3, align_bytes=64)
+            nc.vector.quantize_mx(
+                out=h_codes[pair][:, tiles, :].rearrange("p j c -> p (j c)").bitcast(FP8X4),
+                scales=h_sc[pair][:, tiles, :].rearrange("p j c -> p (j c)"),
+                in_=h_int[pair][:, tiles, :].rearrange("p j c -> p (j c)"),
+            )
 
-        def gradient(n, half):
-            s2[n, half] = psum.tile([P, BANK], F32, name="s2", bufs=2)
+        def gradient(n, half, banks="s2"):
+            s2[n, half] = psum.tile([P, BANK], F32, name=banks, bufs=2)
+            pair = 2 * (n // TILES) + half
             for g in range(2):
-                piece = 4 * (n // TILES) + 2 * half + g
                 nc.tensor.matmul_mx(
                     out=s2[n, half][:],
-                    lhsT=h_codes[n][:, P * g : P * (g + 1)].bitcast(FP8X4),
-                    lhsT_scale=h_sc[n][:, P * g : P * (g + 1)],
-                    rhs=e_codes[piece][:].bitcast(FP8X4),
-                    rhs_scale=e_sc[piece][:],
+                    lhsT=h_codes[n // 2][:, n % 2, P * g : P * (g + 1)].bitcast(FP8X4),
+                    lhsT_scale=h_sc[n // 2][:, n % 2, P * g : P * (g + 1)],
+                    rhs=e_codes[pair][:, g, :].bitcast(FP8X4),
+                    rhs_scale=e_sc[pair][:, g, :],
                     start=(g == 0),
                     stop=(g == 1),
                 )
 
         def add_running(n, half):
             if half == 0:
-                t_sum[n] = work.tile([P, V], F32, name="t_sum", bufs=2)
+                t_sum[n] = work.tile([P, V], F32, name="t_sum", bufs=4)
             cols = slice(BANK * half, BANK * (half + 1))
             nc.vector.scalar_tensor_tensor(
                 out=t_sum[n][:, cols], in0=run[n][:, cols], scalar=BETA, in1=s2[n, half][:], op0=MULT, op1=ADD
@@ -219,7 +226,7 @@ def tile_grouped_unembedding_gradient_k7_kernel(
 
         def round_y(n, groups, copy):
             if groups.start == 0:
-                y_bf[n] = work.tile([P, V], BF16, name="y_bf", bufs=2)
+                y_bf[n] = work.tile([P, V], BF16, name="y_bf", bufs=4)
             copy(
                 out=y_bf[n][:].rearrange("p (g u m e) -> p g u m e", g=2, u=2, e=2)[:, groups],
                 in_=y[n][:].rearrange("p (g m u e) -> p g u m e", g=2, u=2, e=2)[:, groups],
@@ -250,11 +257,11 @@ def tile_grouped_unembedding_gradient_k7_kernel(
                 in_=y_int[h][:, g, 4 * cols.start : 4 * cols.stop],
             )
 
-        def store_codes(h, cols):
+        def store_codes(h, groups, cols):
             rows = out_1.rearrange("g p m t -> p g (m t)")
             nc.sync.dma_start(
-                out=rows[:, :, 4 * (D * h + cols.start) : 4 * (D * h + cols.stop)].bitcast(I32),
-                in_=y_codes[h][:, :, cols].bitcast(I32),
+                out=rows[:, groups, 4 * (D * h + cols.start) : 4 * (D * h + cols.stop)].bitcast(I32),
+                in_=y_codes[h][:, groups, cols].bitcast(I32),
             )
 
         def store_scales(cols):
@@ -266,6 +273,7 @@ def tile_grouped_unembedding_gradient_k7_kernel(
 
         both, whole = slice(0, 2), slice(0, V)
         halves = [slice(0, BANK), slice(BANK, V)]
+        first, second = slice(0, 1), slice(1, 2)
         nc.vector.memset(vec_rows[:], 0.0)
         nc.vector.memset(bias_rows[:], 0.0)
         nc.vector.memset(a_sc[:].bitcast(I32), 0)
@@ -276,26 +284,30 @@ def tile_grouped_unembedding_gradient_k7_kernel(
                 in_=vec.rearrange("h (q w) -> (h q) w", q=4),
             )
         nc.sync.dma_start(out=bias_raw[:], in_=bias.rearrange("h (j p) -> (h j) p", p=P))
-        for j in range(8):
+        for j in range(7):
             load_x(j)
 
         vec_bank = psum.tile([P, 4, P], F32, name="tr", bufs=4)
         nc.tensor.transpose(vec_bank[:, 0, :], vec_rows[:], ident[:])
         nc.vector.tensor_copy(out=vec_cols[:], in_=vec_bank[:, 0, : RATE_ROW + 4 * G])
         nc.vector.tensor_copy(out=bias_rows[:UNITS, :], in_=bias_raw[:])
+        spread(0, "s1", 2)
         for j in range(8):
             sort_x(j)
+            if j == 0:
+                load_x(7)
             turn_x(j)
             if j == 0:
                 bias_bank = psum.tile([P, 4, P], F32, name="tr", bufs=4)
                 nc.tensor.transpose(bias_bank[:, 0, :], bias_rows[:], ident[:])
             if j == 5:
-                spread(0, "s2", 2)
+                spread(RATE_ROW, "s2", 2)
             if j == 1:
+                gather_weight(0, nc.vector.tensor_copy)
                 nc.vector.tensor_copy(out=bias_cols[:], in_=bias_bank[:, 0, :UNITS])
         quantize_x(0, 0)
         quantize_x(0, 1)
-        gather_weight(0, nc.vector.tensor_copy)
+        gather_rate(0, nc.vector.tensor_copy)
         for q in range(4):
             nc.sync.dma_start(
                 out=a_sc[32 * q : 32 * q + 4, :, :].bitcast(I32),
@@ -310,10 +322,11 @@ def tile_grouped_unembedding_gradient_k7_kernel(
         load_running(1)
         quantize_x(1, 0)
         quantize_x(1, 1)
-        interleave_err(0)
+        interleave_err(0, nc.scalar.copy)
         load_err(1, 0, whole)
         load_running(2)
-        interleave_err(1)
+        load_running(3)
+        interleave_err(1, nc.scalar.copy)
         load_err(1, 1, whole)
         project(0, 0, "s1")
         project(1, 0, "s2")
@@ -327,130 +340,125 @@ def tile_grouped_unembedding_gradient_k7_kernel(
             project(n + 2, 1, ("s1", "s2")[n])
             turn_h(n)
             gather_h(n)
-        quantize_err(0)
-        spread(RATE_ROW)
         spread(4)
-        interleave_err(3)
-        gather_rate(0, nc.scalar.copy)
-        gather_weight(1, nc.scalar.copy)
+        interleave_err(3, nc.scalar.copy)
         weigh(2, 0)
         weigh(3, 0)
         project(LEAD, 0)
         weigh(2, 1)
         weigh(3, 1)
-        quantize_err(1)
-        quantize_h(0)
-        gradient(0, 0)
-        project(LEAD, 1)
-        interleave_err(2)
         turn_h(2)
+        project(LEAD, 1)
         turn_h(3)
+        quantize_err(0, both)
+        quantize_h(0, both)
+        gradient(0, 0)
+        interleave_err(2, nc.vector.tensor_copy)
         gather_h(2)
         gather_h(3)
-        quantize_h(1)
-        quantize_err(2)
-        quantize_err(3)
+        gather_weight(1, nc.vector.tensor_copy)
+        quantize_err(1, both)
         gradient(0, 1)
+        quantize_h(1, both)
+        for h in range(1, G):
+            spread(RATE_ROW + 4 * h)
 
         last = UNITS - 1
-        first, second = slice(0, 1), slice(1, 2)
-
-        def finish_head(h):
-            quantize_y(h, 0, slice(0, D))
-            quantize_y(h, 1, slice(0, D))
-            store_codes(h, slice(0, D))
-
-        for s in range(UNITS - LEAD):
+        for s in range(0, UNITS - LEAD, 2):
             ahead = s + LEAD
-            if s in (0, 1, 4, 5):
-                load_err(s // TILES + 2, s % 2, whole)
-            load_running(s + 3)
-            if s in (1, 5):
+            if s % TILES == 0 and s // TILES + 2 < G:
+                load_err(s // TILES + 2, 0, whole)
                 load_stage1(s // TILES + 2)
-            interleave_err(ahead)
-            add_running(s, 0)
-            scale(s, halves[0], nc.gpsimd)
-            gradient(s + 1, 0)
-            if s >= 1:
-                round_y(s - 1, both, nc.scalar.copy)
-            add_running(s, 1)
-            scale(s, slice(BANK, GPSIMD_COLS), nc.gpsimd)
+                load_err(s // TILES + 2, 1, whole)
+            load_running(s + 4)
+            interleave_err(ahead, nc.scalar.copy)
+            interleave_err(ahead + 1, nc.scalar.copy)
+            if s == 0:
+                for h in range(1, G):
+                    gather_rate(h, nc.scalar.copy)
+            for n in (s, s + 1):
+                for half in range(2):
+                    add_running(n, half)
+                    scale(n, halves[half], nc.gpsimd)
+                    if n == s or half == 0:
+                        gradient(n + 1, half)
+                store_y(n, whole)
+                if n == s:
+                    load_running(s + 5)
+                    for half in range(2):
+                        weigh(ahead, half)
+                        project(ahead + 1, half)
             if s >= 2:
                 turn_y(s - 2, both)
+                turn_y(s - 1, both)
             else:
-                spread(4 * (s + 2))
-                spread(RATE_ROW + 4 * (s + 1))
-                gather_rate(s + 1, nc.scalar.copy)
-            weigh(ahead, 0)
-            if ahead < last:
-                project(ahead + 1, 0)
-            weigh(ahead, 1)
-            turn_h(ahead)
-            if ahead < last:
-                project(ahead + 1, 1)
-            gather_h(ahead)
+                spread(8)
+                spread(12)
+            weigh(ahead + 1, 0)
+            if ahead + 2 < UNITS:
+                project(ahead + 2, 0)
+            weigh(ahead + 1, 1)
             if s >= 2:
                 gather_y(s - 2, both, nc.vector.tensor_copy)
+                gather_y(s - 1, both, nc.vector.tensor_copy)
             else:
-                gather_weight(s + 2, nc.vector.tensor_copy)
-            scale(s, slice(GPSIMD_COLS, V))
-            store_y(s, whole)
-            quantize_err(ahead)
-            gradient(s + 1, 1)
-            if s == 0:
-                quantize_h(2)
-            quantize_h(ahead - 1)
-            if s in (6, 10):
-                finish_head((s - 3) // TILES)
+                gather_weight(2, nc.vector.tensor_copy)
+                gather_weight(3, nc.vector.tensor_copy)
+            turn_h(ahead)
+            turn_h(ahead + 1)
+            if ahead + 2 < UNITS:
+                project(ahead + 2, 1)
+            else:
+                gradient(s + 3, 0, "s1")
+            gather_h(ahead)
+            gather_h(ahead + 1)
+            round_y(s, both, nc.scalar.copy)
+            if s >= TILES:
+                round_y(s + 1, both, nc.scalar.copy)
+            quantize_err(ahead // 2, both)
+            gradient(s + 2, 1)
+            if ahead + 2 == UNITS:
+                gradient(s + 3, 1, "s1")
+            if s >= TILES:
+                h, g = (s - TILES) // TILES, s % TILES // 2
+                quantize_y(h, g, slice(0, D))
+                store_codes(h, slice(g, g + 1), slice(0, D))
+            else:
+                round_y(s + 1, both, nc.vector.tensor_copy)
+            quantize_h(ahead // 2, both)
 
-        s = UNITS - LEAD
-        load_running(last)
-        round_y(s - 1, both, nc.scalar.copy)
-        spread(RATE_ROW + 4 * (G - 1))
-        turn_y(s - 2, both)
-        gather_rate(G - 1, nc.scalar.copy)
-        gather_y(s - 2, both, nc.scalar.copy)
-        for s in range(UNITS - LEAD, UNITS):
-            add_running(s, 0)
-            if s < last:
-                gradient(s + 1, 0)
-            if s == UNITS - LEAD:
-                quantize_h(last)
-                turn_y(s - 1, both)
-                gather_y(s - 1, both, nc.scalar.copy)
-            else:
-                scale(s - 1, halves[1])
-                store_y(s - 1, whole)
-                turn_y(s - 1, first)
-                round_y(s - 1, second, nc.scalar.copy)
-                gather_y(s - 1, first, nc.scalar.copy)
-            add_running(s, 1)
-            if s < last:
-                gradient(s + 1, 1)
-            scale(s, halves[0])
-            if s > UNITS - LEAD:
-                turn_y(s - 1, second)
-            round_y(s, first, nc.scalar.copy)
-            if s > UNITS - LEAD:
-                gather_y(s - 1, second, nc.scalar.copy)
-            if s == UNITS - LEAD + 1:
-                finish_head(G - 2)
-                store_scales(slice(0, D * (G - 1)))
         h = G - 1
-        store_y(last, halves[0])
-        quantize_y(h, 0, slice(0, 2 * P))
-        scale(last, halves[1])
-        store_y(last, halves[1])
-        turn_y(last, first)
-        quantize_y(h, 1, slice(0, 2 * P))
-        round_y(last, second, nc.vector.tensor_copy)
-        turn_y(last, second)
-        gather_y(last, first, nc.scalar.copy)
+        base = UNITS - LEAD
+        order = [(n + j, half) for n in (base, base + 2) for half in range(2) for j in range(2)]
+        groups = (first, second)
+        turn_y(base - 2, both)
+        turn_y(base - 1, both)
+        gather_y(base - 2, both, nc.scalar.copy)
+        gather_y(base - 1, both, nc.scalar.copy)
+        for i, (n, half) in enumerate(order):
+            add_running(n, half)
+            if i < GPSIMD_HALVES:
+                scale(n, halves[half], nc.gpsimd)
+                store_y(n, halves[half])
+            if i + 4 < len(order):
+                gradient(*order[i + 4], ("s2", "s1")[i % 2])
+        for g in range(2):
+            quantize_y(h - 1, g, slice(0, D))
+        store_codes(h - 1, both, slice(0, D))
+        for i, (n, half) in enumerate(order):
+            if i >= GPSIMD_HALVES:
+                scale(n, halves[half])
+                store_y(n, halves[half])
+            round_y(n, groups[half], nc.scalar.copy if i < SCALAR_ROUNDS else nc.vector.tensor_copy)
+            turn_y(n, groups[half])
+            if i >= 1:
+                gather_y(order[i - 1][0], groups[order[i - 1][1]], nc.scalar.copy)
+        store_scales(slice(0, D * (G - 1)))
+        quantize_y(h, 0, slice(0, D))
         gather_y(last, second, nc.scalar.copy)
-        quantize_y(h, 0, slice(2 * P, 3 * P))
+        quantize_y(h, 1, slice(0, 2 * P))
+        store_codes(h, first, slice(0, D))
         quantize_y(h, 1, slice(2 * P, 3 * P))
-        store_codes(h, slice(0, 3 * P))
-        quantize_y(h, 0, slice(3 * P, 4 * P))
         quantize_y(h, 1, slice(3 * P, 4 * P))
-        store_codes(h, slice(3 * P, 4 * P))
+        store_codes(h, second, slice(0, D))
         store_scales(slice(D * (G - 1), G * D))

@@ -18,14 +18,16 @@ ADD = mybir.AluOpType.add
 MULT = mybir.AluOpType.mult
 
 P = 128
-PASS = 512
+GROUP = 512
 BANK = 512
-TILES = D // P
-UNITS = G * TILES
-LEAD = 4
+PACK = 4
+HEAD_TILES = D // P
+TILES = G * HEAD_TILES
+X_BLOCKS = T // P
+LEAD = HEAD_TILES
+VEC_ROWS = T // (2 * P)
 RATE_ROW = 32
-GPSIMD_HALVES = 3
-SCALAR_ROUNDS = 6
+GPSIMD_LAST_HALVES = 2
 
 
 def tile_grouped_unembedding_gradient_k7_kernel(
@@ -39,118 +41,138 @@ def tile_grouped_unembedding_gradient_k7_kernel(
         ctx.enter_context(tc.manual_schedule())
 
         ident = keep.tile([P, P], F32, name="ident")
+        bias_raw = keep.tile([TILES, P], BF16, name="bias_raw")
         bias_rows = keep.tile([P, P], F32, name="bias_rows")
-        bias_raw = keep.tile([UNITS, P], BF16, name="bias_raw")
+        bias_cols = keep.tile([P, TILES], F32, name="bias_cols")
         vec_rows = keep.tile([P, P], F32, name="vec_rows")
-        vec_cols = keep.tile([P, RATE_ROW + 4 * G], F32, name="vec_cols")
-        bias_cols = keep.tile([P, UNITS], F32, name="bias_cols")
+        vec_cols = keep.tile([P, RATE_ROW + G * VEC_ROWS], F32, name="vec_cols")
         a_sc = keep.tile([P, 2 * G, D], U8, name="a_sc", align_bytes=64)
-        y_sc = keep.tile([P, 2, G * D], U8, name="y_sc", align_bytes=64)
         x_codes = keep.tile([P, 2, T], U32, name="x_codes", align_bytes=64)
         x_sc = keep.tile([P, 2, T], U8, name="x_sc", align_bytes=64)
 
-        x_raw, x_int, a_w, tw, rt, run, e_raw, e_int, e_codes, e_sc = {}, {}, {}, {}, {}, {}, {}, {}, {}, {}
-        x_srt, spread_bank = {}, {}
-        s1, h_t, h_tr, h_int, h_codes, h_sc = {}, {}, {}, {}, {}, {}
-        s2, t_sum, y, y_bf, y_tr, y_int, y_codes = {}, {}, {}, {}, {}, {}, {}
+        x_raw, x_sorted, x_staged, a_w, weight_bc, rate_bc, spread_bank = {}, {}, {}, {}, {}, {}, {}
+        run, e_raw, e_staged, e_codes, e_sc = {}, {}, {}, {}, {}
+        mm1, h_t, h_bank, h_staged, h_codes, h_sc = {}, {}, {}, {}, {}, {}
+        mm2, total, y, y_bf, y_bank, y_staged, y_codes, y_sc = {}, {}, {}, {}, {}, {}, {}, {}
 
-        def load_x(j):
-            x_raw[j] = work.tile([P, K], BF16, name="x_raw", bufs=7)
-            nc.sync.dma_start(out=x_raw[j][:], in_=x[P * j : P * (j + 1), :])
+        halves = (slice(0, BANK), slice(BANK, 2 * BANK))
+        whole = slice(0, V)
+        one_group = (slice(0, 1), slice(1, 2))
+        both_groups = slice(0, 2)
 
-        def load_stage1(h):
+        def transpose_bank(banks="tr"):
+            return psum.tile([P, 4, P], F32, name=banks, bufs=4 if banks == "tr" else 2)
+
+
+        def load_x(b):
+            x_raw[b] = work.tile([P, K], BF16, name="x_raw", bufs=X_BLOCKS)
+            nc.sync.dma_start(out=x_raw[b][:], in_=x[P * b : P * (b + 1), :])
+
+        def load_a_words(h):
             a_w[h] = work.tile([P, 2, 2 * D], U8, name="a_w", bufs=2, align_bytes=64)
-            nc.sync.dma_start(
-                out=a_w[h][:].bitcast(I32),
-                in_=a_words[2 * h : 2 * h + 2].rearrange("g p n -> p g n").bitcast(I32),
-            )
+            words = a_words[2 * h : 2 * h + 2].rearrange("g p n -> p g n")
+            nc.sync.dma_start(out=a_w[h][:].bitcast(I32), in_=words.bitcast(I32))
+
+        def load_a_scales(heads):
+            groups = slice(2 * heads.start, 2 * heads.stop)
+            for quad in range(4):
+                rows = a_scales[groups, 4 * quad : 4 * quad + 4, :].rearrange("g r n -> r g n")
+                nc.sync.dma_start(out=a_sc[32 * quad : 32 * quad + 4, groups, :].bitcast(I32), in_=rows.bitcast(I32))
 
         def load_err(h, g, cols):
-            raw = work.tile([P, 4, cols.stop - cols.start], BF16, name="e_raw", bufs=4)
-            rows = err[h, PASS * g : PASS * (g + 1), cols]
-            nc.sync.dma_start(out=raw[:], in_=rows.rearrange("(p j) v -> p j v", j=4))
-            for first in range(cols.start, cols.stop, BANK):
-                offset = first - cols.start
-                e_raw[4 * h + 2 * (first // BANK) + g] = raw[:, :, offset : offset + BANK]
+            raw = work.tile([P, PACK, cols.stop - cols.start], BF16, name="e_raw", bufs=4)
+            rows = err[h, GROUP * g : GROUP * (g + 1), cols]
+            nc.sync.dma_start(out=raw[:], in_=rows.rearrange("(p t) v -> p t v", t=PACK))
+            for start in range(cols.start, cols.stop, BANK):
+                e_raw[h, start // BANK, g] = raw[:, :, start - cols.start : start - cols.start + BANK]
 
         def load_running(n):
-            h, j = divmod(n, TILES)
+            h, j = divmod(n, HEAD_TILES)
             run[n] = work.tile([P, V], BF16, name="run", bufs=5)
             nc.sync.dma_start(out=run[n][:], in_=running[h, P * j : P * (j + 1), :])
 
-        def spread(first_row, banks="tr", bufs=4):
-            spread_bank[first_row] = psum.tile([P, 4, P], F32, name=banks, bufs=bufs)
-            for q in range(4):
+
+        def spread(first_row, banks="tr"):
+            spread_bank[first_row] = transpose_bank(banks)
+            for q in range(VEC_ROWS):
                 column = vec_cols[:, first_row + q : first_row + q + 1]
                 nc.tensor.transpose(spread_bank[first_row][:, q, :], column.to_broadcast([P, P]), ident[:])
 
+        def spread_weight(h, banks="tr"):
+            spread(VEC_ROWS * h, banks)
+
+        def spread_rate(h, banks="tr"):
+            spread(RATE_ROW + VEC_ROWS * h, banks)
+
         def gather_weight(h, copy):
-            tw[h] = work.tile([P, T], BF16, name="tw", bufs=G)
-            words = spread_bank[4 * h][:].rearrange("p q w -> p (q w)")
+            weight_bc[h] = work.tile([P, T], BF16, name="weight_bc", bufs=G)
+            pairs = spread_bank[VEC_ROWS * h][:].rearrange("c q w -> c (q w)")
             copy(
-                out=tw[h][:].bitcast(F32).rearrange("p (g u m) -> p g u m", g=2, u=2),
-                in_=words.rearrange("p (g m u) -> p g u m", g=2, u=2),
+                out=weight_bc[h][:].bitcast(F32).rearrange("c (g u p) -> c g u p", g=2, u=2),
+                in_=pairs.rearrange("c (g p u) -> c g u p", g=2, u=2),
             )
 
         def gather_rate(h, copy):
-            rt[h] = work.tile([P, V], BF16, name="rt", bufs=G)
-            copy(out=rt[h][:].bitcast(F32), in_=spread_bank[RATE_ROW + 4 * h][:].rearrange("p q w -> p (q w)"))
+            rate_bc[h] = work.tile([P, V], BF16, name="rate_bc", bufs=G)
+            pairs = spread_bank[RATE_ROW + VEC_ROWS * h][:].rearrange("c q w -> c (q w)")
+            copy(out=rate_bc[h][:].bitcast(F32), in_=pairs)
 
-        def sort_x(j):
-            x_srt[j] = work.tile([P, 4, P], F32, name="x_srt", bufs=3)
+
+        def sort_x(b):
+            x_sorted[b] = work.tile([P, 4, P], F32, name="x_sorted", bufs=3)
             nc.vector.tensor_copy(
-                out=x_srt[j][:].rearrange("p (g u) m -> p g u m", u=2),
-                in_=x_raw[j][:].bitcast(F32).rearrange("p (g m u) -> p g u m", g=2, u=2),
+                out=x_sorted[b][:].rearrange("r (g u) p -> r g u p", u=2),
+                in_=x_raw[b][:].bitcast(F32).rearrange("r (g p u) -> r g u p", g=2, u=2),
             )
 
-        def turn_x(j):
-            half = j // 4
-            if j % 4 == 0:
-                x_int[half] = work.tile([P, 2, PASS * 4], BF16, name="staged", bufs=3, align_bytes=64)
-            bank = psum.tile([P, 4, P], F32, name="tr", bufs=4)
+        def turn_x(b):
+            half, j = divmod(b, 4)
+            if j == 0:
+                x_staged[half] = work.tile([P, 2, BANK * PACK], BF16, name="staged", bufs=3, align_bytes=64)
+            bank = transpose_bank()
             for q in range(4):
-                nc.tensor.transpose(bank[:, q, :], x_srt[j][:, q, :], ident[:])
-            dst = x_int[half][:].bitcast(F32).rearrange("p g (u j m e w) -> p g j u m e w", u=2, j=4, e=2, w=2)
-            src = bank[:].rearrange("p (g w) (m u e) -> p g u m e w", w=2, u=2, e=2)
+                nc.tensor.transpose(bank[:, q, :], x_sorted[b][:, q, :], ident[:])
+            dst = x_staged[half][:].bitcast(F32).rearrange("c g (u j m e w) -> c g j u m e w", u=2, j=4, e=2, w=2)
+            src = bank[:].rearrange("c (g w) (m u e) -> c g u m e w", w=2, u=2, e=2)
             for g in range(2):
-                nc.scalar.copy(out=dst[:, g, j % 4], in_=src[:, g])
+                nc.scalar.copy(out=dst[:, g, j], in_=src[:, g])
 
         def quantize_x(half, g):
-            cols = slice(PASS * half, PASS * (half + 1))
             nc.vector.quantize_mx(
-                out=x_codes[:, g, cols].bitcast(FP8X4), scales=x_sc[:, g, cols], in_=x_int[half][:, g, :]
+                out=x_codes[:, g, halves[half]].bitcast(FP8X4),
+                scales=x_sc[:, g, halves[half]],
+                in_=x_staged[half][:, g, :],
             )
 
-        def interleave_err(piece, copy):
-            pair, g = divmod(piece, 2)
-            if pair not in e_int:
-                e_int[pair] = work.tile([P, 2, BANK * 4], BF16, name="staged", bufs=3, align_bytes=64)
+
+        def interleave_err(h, half, g, copy):
+            if (h, half) not in e_staged:
+                e_staged[h, half] = work.tile([P, 2, BANK * PACK], BF16, name="staged", bufs=3, align_bytes=64)
             copy(
-                out=e_int[pair][:, g, :].rearrange("p (c i t) -> p c t i", i=4, t=4),
-                in_=e_raw[piece].rearrange("p t (c i) -> p c t i", i=4),
+                out=e_staged[h, half][:, g, :].rearrange("p (c i t) -> p c t i", i=4, t=PACK),
+                in_=e_raw[h, half, g].rearrange("p t (c i) -> p c t i", i=4),
             )
 
-        def quantize_err(pair, groups):
-            if groups.start == 0:
-                e_codes[pair] = work.tile([P, 2, BANK], U32, name="e_codes", bufs=4, align_bytes=64)
-                e_sc[pair] = work.tile([P, 2, BANK], U8, name="e_sc", bufs=4, align_bytes=64)
+        def quantize_err(h, half):
+            e_codes[h, half] = work.tile([P, 2, BANK], U32, name="e_codes", bufs=4, align_bytes=64)
+            e_sc[h, half] = work.tile([P, 2, BANK], U8, name="e_sc", bufs=4, align_bytes=64)
             nc.vector.quantize_mx(
-                out=e_codes[pair][:, groups, :].rearrange("p g c -> p (g c)").bitcast(FP8X4),
-                scales=e_sc[pair][:, groups, :].rearrange("p g c -> p (g c)"),
-                in_=e_int[pair][:, groups, :].rearrange("p g c -> p (g c)"),
+                out=e_codes[h, half][:].rearrange("p g c -> p (g c)").bitcast(FP8X4),
+                scales=e_sc[h, half][:].rearrange("p g c -> p (g c)"),
+                in_=e_staged[h, half][:].rearrange("p g c -> p (g c)"),
             )
 
-        def project(n, half, banks="s1"):
-            h, j = divmod(n, TILES)
-            s1[n, half] = psum.tile([P, BANK], F32, name=banks, bufs=2)
-            cols = slice(BANK * half, BANK * (half + 1))
+
+        def project(n, half, banks="mm1"):
+            h, j = divmod(n, HEAD_TILES)
+            mm1[n, half] = psum.tile([P, BANK], F32, name=banks, bufs=2)
             for g in range(2):
                 nc.tensor.matmul_mx(
-                    out=s1[n, half][:],
+                    out=mm1[n, half][:],
                     lhsT=a_w[h][:, g, 2 * P * j : 2 * P * (j + 1)].bitcast(FP4X4),
                     lhsT_scale=a_sc[:, 2 * h + g, P * j : P * (j + 1)],
-                    rhs=x_codes[:, g, cols].bitcast(FP8X4),
-                    rhs_scale=x_sc[:, g, cols],
+                    rhs=x_codes[:, g, halves[half]].bitcast(FP8X4),
+                    rhs_scale=x_sc[:, g, halves[half]],
                     start=(g == 0),
                     stop=(g == 1),
                 )
@@ -158,190 +180,187 @@ def tile_grouped_unembedding_gradient_k7_kernel(
         def weigh(n, half):
             if half == 0:
                 h_t[n] = work.tile([P, T], BF16, name="h_t", bufs=LEAD)
-            cols = slice(BANK * half, BANK * (half + 1))
             nc.vector.scalar_tensor_tensor(
-                out=h_t[n][:, cols],
-                in0=s1[n, half][:],
+                out=h_t[n][:, halves[half]],
+                in0=mm1[n, half][:],
                 scalar=bias_cols[:, n : n + 1],
-                in1=tw[n // TILES][:, cols],
+                in1=weight_bc[n // HEAD_TILES][:, halves[half]],
                 op0=ADD,
                 op1=MULT,
             )
 
         def turn_h(n):
-            words = h_t[n][:].bitcast(F32)
-            h_tr[n] = psum.tile([P, 4, P], F32, name="tr", bufs=4)
+            pairs = h_t[n][:].bitcast(F32)
+            h_bank[n] = transpose_bank()
             for q in range(4):
-                nc.tensor.transpose(h_tr[n][:, q, :], words[:, P * q : P * (q + 1)], ident[:])
+                nc.tensor.transpose(h_bank[n][:, q, :], pairs[:, P * q : P * (q + 1)], ident[:])
 
         def gather_h(n):
             if n % 2 == 0:
-                h_int[n // 2] = work.tile([P, 2, T], BF16, name="h_int", bufs=2, align_bytes=64)
+                h_staged[n // 2] = work.tile([P, 2, T], BF16, name="h_staged", bufs=2, align_bytes=64)
             nc.scalar.copy(
-                out=h_int[n // 2][:, n % 2, :].bitcast(F32).rearrange("p (g d u) -> p g d u", g=2, u=2),
-                in_=h_tr[n][:].rearrange("p (g u) d -> p g d u", u=2),
+                out=h_staged[n // 2][:, n % 2, :].bitcast(F32).rearrange("p (g d u) -> p g d u", g=2, u=2),
+                in_=h_bank[n][:].rearrange("p (g u) d -> p g d u", u=2),
             )
 
-        def quantize_h(pair, tiles):
-            if tiles.start == 0:
-                h_codes[pair] = work.tile([P, 2, 2 * P], U32, name="h_codes", bufs=3, align_bytes=64)
-                h_sc[pair] = work.tile([P, 2, 2 * P], U8, name="h_sc", bufs=3, align_bytes=64)
+        def quantize_h(n):
+            couple = n // 2
+            h_codes[couple] = work.tile([P, 2, 2 * P], U32, name="h_codes", bufs=3, align_bytes=64)
+            h_sc[couple] = work.tile([P, 2, 2 * P], U8, name="h_sc", bufs=3, align_bytes=64)
             nc.vector.quantize_mx(
-                out=h_codes[pair][:, tiles, :].rearrange("p j c -> p (j c)").bitcast(FP8X4),
-                scales=h_sc[pair][:, tiles, :].rearrange("p j c -> p (j c)"),
-                in_=h_int[pair][:, tiles, :].rearrange("p j c -> p (j c)"),
+                out=h_codes[couple][:].rearrange("p j c -> p (j c)").bitcast(FP8X4),
+                scales=h_sc[couple][:].rearrange("p j c -> p (j c)"),
+                in_=h_staged[couple][:].rearrange("p j c -> p (j c)"),
             )
 
-        def gradient(n, half, banks="s2"):
-            s2[n, half] = psum.tile([P, BANK], F32, name=banks, bufs=2)
-            pair = 2 * (n // TILES) + half
+
+        def gradient(n, half, banks="mm2"):
+            h = n // HEAD_TILES
+            mm2[n, half] = psum.tile([P, BANK], F32, name=banks, bufs=2)
             for g in range(2):
                 nc.tensor.matmul_mx(
-                    out=s2[n, half][:],
+                    out=mm2[n, half][:],
                     lhsT=h_codes[n // 2][:, n % 2, P * g : P * (g + 1)].bitcast(FP8X4),
                     lhsT_scale=h_sc[n // 2][:, n % 2, P * g : P * (g + 1)],
-                    rhs=e_codes[pair][:, g, :].bitcast(FP8X4),
-                    rhs_scale=e_sc[pair][:, g, :],
+                    rhs=e_codes[h, half][:, g, :].bitcast(FP8X4),
+                    rhs_scale=e_sc[h, half][:, g, :],
                     start=(g == 0),
                     stop=(g == 1),
                 )
 
         def add_running(n, half):
             if half == 0:
-                t_sum[n] = work.tile([P, V], F32, name="t_sum", bufs=4)
-            cols = slice(BANK * half, BANK * (half + 1))
+                total[n] = work.tile([P, V], F32, name="total", bufs=HEAD_TILES)
             nc.vector.scalar_tensor_tensor(
-                out=t_sum[n][:, cols], in0=run[n][:, cols], scalar=BETA, in1=s2[n, half][:], op0=MULT, op1=ADD
+                out=total[n][:, halves[half]],
+                in0=run[n][:, halves[half]],
+                scalar=BETA,
+                in1=mm2[n, half][:],
+                op0=MULT,
+                op1=ADD,
             )
 
-        def scale(n, cols, engine=nc.vector):
-            h, j = divmod(n, TILES)
-            if cols.start == 0:
-                y[n] = work.tile([P, V], F32, name="y", bufs=4)
-            engine.tensor_tensor(out=y[n][:, cols], in0=t_sum[n][:, cols], in1=rt[h][:, cols], op=MULT)
+        def scale(n, half, engine):
+            if half == 0:
+                y[n] = work.tile([P, V], F32, name="y", bufs=HEAD_TILES)
+            cols = halves[half]
+            engine.tensor_tensor(
+                out=y[n][:, cols], in0=total[n][:, cols], in1=rate_bc[n // HEAD_TILES][:, cols], op=MULT
+            )
 
         def store_y(n, cols):
-            h, j = divmod(n, TILES)
+            h, j = divmod(n, HEAD_TILES)
             nc.sync.dma_start(out=out_0[h, P * j : P * (j + 1), cols], in_=y[n][:, cols])
+
 
         def round_y(n, groups, copy):
             if groups.start == 0:
-                y_bf[n] = work.tile([P, V], BF16, name="y_bf", bufs=4)
+                y_bf[n] = work.tile([P, V], BF16, name="y_bf", bufs=HEAD_TILES)
             copy(
-                out=y_bf[n][:].rearrange("p (g u m e) -> p g u m e", g=2, u=2, e=2)[:, groups],
-                in_=y[n][:].rearrange("p (g m u e) -> p g u m e", g=2, u=2, e=2)[:, groups],
+                out=y_bf[n][:].rearrange("d (g u p e) -> d g u p e", g=2, u=2, e=2)[:, groups],
+                in_=y[n][:].rearrange("d (g p u e) -> d g u p e", g=2, u=2, e=2)[:, groups],
             )
 
         def turn_y(n, groups):
-            words = y_bf[n][:].bitcast(F32)
-            y_tr[n, groups.start] = psum.tile([P, 4, P], F32, name="tr", bufs=4)
+            pairs = y_bf[n][:].bitcast(F32)
+            y_bank[n, groups.start] = transpose_bank()
             for q in range(2 * groups.start, 2 * groups.stop):
-                nc.tensor.transpose(y_tr[n, groups.start][:, q, :], words[:, P * q : P * (q + 1)], ident[:])
+                nc.tensor.transpose(y_bank[n, groups.start][:, q, :], pairs[:, P * q : P * (q + 1)], ident[:])
 
         def gather_y(n, groups, copy):
-            h, j = divmod(n, TILES)
+            h, j = divmod(n, HEAD_TILES)
             if j == 0 and groups.start == 0:
-                y_int[h] = work.tile([P, 2, D * 4], BF16, name="y_int", bufs=2, align_bytes=64)
-            dst = y_int[h][:].bitcast(F32).rearrange("p g (d u) -> p g d u", u=2)
+                y_staged[h] = work.tile([P, 2 * D * PACK], BF16, name="y_staged", bufs=2, align_bytes=64)
+            dst = y_staged[h][:].bitcast(F32).rearrange("p (g d u) -> p g d u", g=2, u=2)
             copy(
                 out=dst[:, groups, P * j : P * (j + 1), :],
-                in_=y_tr[n, groups.start][:].rearrange("p (g u) d -> p g d u", u=2)[:, groups],
+                in_=y_bank[n, groups.start][:].rearrange("p (g u) d -> p g d u", u=2)[:, groups],
             )
 
-        def quantize_y(h, g, cols):
-            if g == 0 and cols.start == 0:
-                y_codes[h] = work.tile([P, 2, D], U32, name="y_codes", bufs=2, align_bytes=64)
+        def quantize_y(h, g):
+            if g == 0:
+                y_sc[h] = work.tile([P, 2 * D], U8, name="y_sc", bufs=2, align_bytes=64)
+            y_codes[h, g] = work.tile([P, D], U32, name="y_codes", bufs=4, align_bytes=64)
             nc.vector.quantize_mx(
-                out=y_codes[h][:, g, cols].bitcast(FP8X4),
-                scales=y_sc[:, g, D * h + cols.start : D * h + cols.stop],
-                in_=y_int[h][:, g, 4 * cols.start : 4 * cols.stop],
+                out=y_codes[h, g][:].bitcast(FP8X4),
+                scales=y_sc[h][:, D * g : D * (g + 1)],
+                in_=y_staged[h][:, PACK * D * g : PACK * D * (g + 1)],
             )
+            rows = out_1[g].rearrange("p m t -> p (m t)")[:, PACK * D * h : PACK * D * (h + 1)]
+            nc.sync.dma_start(out=rows.bitcast(I32), in_=y_codes[h, g][:].bitcast(I32))
 
-        def store_codes(h, groups, cols):
-            rows = out_1.rearrange("g p m t -> p g (m t)")
-            nc.sync.dma_start(
-                out=rows[:, groups, 4 * (D * h + cols.start) : 4 * (D * h + cols.stop)].bitcast(I32),
-                in_=y_codes[h][:, groups, cols].bitcast(I32),
-            )
+        def store_scales(h, queue):
+            for quad in range(4):
+                rows = out_2[:, 4 * quad : 4 * quad + 4, D * h : D * (h + 1)].rearrange("g r m -> r g m")
+                live = y_sc[h][32 * quad : 32 * quad + 4, :].bitcast(I32).rearrange("r (g m) -> r g m", g=2)
+                queue.dma_start(out=rows.bitcast(I32), in_=live)
 
-        def store_scales(cols):
-            for q in range(4):
-                nc.sync.dma_start(
-                    out=out_2[:, 4 * q : 4 * q + 4, cols].rearrange("g r m -> r g m").bitcast(I32),
-                    in_=y_sc[32 * q : 32 * q + 4, :, cols].bitcast(I32),
-                )
 
-        both, whole = slice(0, 2), slice(0, V)
-        halves = [slice(0, BANK), slice(BANK, V)]
-        first, second = slice(0, 1), slice(1, 2)
         nc.vector.memset(vec_rows[:], 0.0)
         nc.vector.memset(bias_rows[:], 0.0)
         nc.vector.memset(a_sc[:].bitcast(I32), 0)
         make_identity(nc, ident[:])
         for first_row, vec in ((0, token_weight), (RATE_ROW, rate)):
             nc.sync.dma_start(
-                out=vec_rows[first_row : first_row + 4 * G, :].bitcast(BF16),
-                in_=vec.rearrange("h (q w) -> (h q) w", q=4),
+                out=vec_rows[first_row : first_row + G * VEC_ROWS, :].bitcast(BF16),
+                in_=vec.rearrange("h (q w) -> (h q) w", q=VEC_ROWS),
             )
         nc.sync.dma_start(out=bias_raw[:], in_=bias.rearrange("h (j p) -> (h j) p", p=P))
-        for j in range(7):
-            load_x(j)
-
-        vec_bank = psum.tile([P, 4, P], F32, name="tr", bufs=4)
-        nc.tensor.transpose(vec_bank[:, 0, :], vec_rows[:], ident[:])
-        nc.vector.tensor_copy(out=vec_cols[:], in_=vec_bank[:, 0, : RATE_ROW + 4 * G])
-        nc.vector.tensor_copy(out=bias_rows[:UNITS, :], in_=bias_raw[:])
-        spread(0, "s1", 2)
-        for j in range(8):
-            sort_x(j)
-            if j == 0:
-                load_x(7)
-            turn_x(j)
-            if j == 0:
-                bias_bank = psum.tile([P, 4, P], F32, name="tr", bufs=4)
-                nc.tensor.transpose(bias_bank[:, 0, :], bias_rows[:], ident[:])
-            if j == 5:
-                spread(RATE_ROW, "s2", 2)
-            if j == 1:
-                gather_weight(0, nc.vector.tensor_copy)
-                nc.vector.tensor_copy(out=bias_cols[:], in_=bias_bank[:, 0, :UNITS])
-        quantize_x(0, 0)
-        quantize_x(0, 1)
-        gather_rate(0, nc.vector.tensor_copy)
-        for q in range(4):
-            nc.sync.dma_start(
-                out=a_sc[32 * q : 32 * q + 4, :, :].bitcast(I32),
-                in_=a_scales[:, 4 * q : 4 * q + 4, :].rearrange("g r n -> r g n").bitcast(I32),
-            )
-        load_stage1(0)
+        for b in range(X_BLOCKS):
+            load_x(b)
+        load_a_scales(slice(0, 1))
+        load_a_words(0)
         for half in range(2):
             for g in range(2):
                 load_err(0, g, halves[half])
         load_running(0)
-        load_stage1(1)
+        load_a_words(1)
+        load_a_scales(slice(1, 2))
         load_running(1)
+
+        vec_bank = transpose_bank()
+        nc.tensor.transpose(vec_bank[:, 0, :], vec_rows[:], ident[:])
+        nc.vector.tensor_copy(out=vec_cols[:], in_=vec_bank[:, 0, : RATE_ROW + G * VEC_ROWS])
+        nc.vector.tensor_copy(out=bias_rows[:TILES, :], in_=bias_raw[:])
+        spread_weight(0, "mm1")
+        sort_x(0)
+        turn_x(0)
+        bias_bank = transpose_bank()
+        nc.tensor.transpose(bias_bank[:, 0, :], bias_rows[:], ident[:])
+        sort_x(1)
+        turn_x(1)
+        gather_weight(0, nc.vector.tensor_copy)
+        nc.vector.tensor_copy(out=bias_cols[:], in_=bias_bank[:, 0, :TILES])
+        for b in range(2, X_BLOCKS):
+            sort_x(b)
+            if b == X_BLOCKS - 2:
+                spread_rate(0, "mm2")
+            turn_x(b)
+        quantize_x(0, 0)
+        quantize_x(0, 1)
+        gather_rate(0, nc.vector.tensor_copy)
         quantize_x(1, 0)
         quantize_x(1, 1)
-        interleave_err(0, nc.scalar.copy)
+
+        interleave_err(0, 0, 0, nc.scalar.copy)
         load_err(1, 0, whole)
         load_running(2)
         load_running(3)
-        interleave_err(1, nc.scalar.copy)
+        interleave_err(0, 0, 1, nc.scalar.copy)
         load_err(1, 1, whole)
-        project(0, 0, "s1")
-        project(1, 0, "s2")
-        project(0, 1, "s1")
-        project(1, 1, "s2")
-        for n in range(2):
-            weigh(n, 0)
-            project(n + 2, 0, ("s1", "s2")[n])
-        for n in range(2):
-            weigh(n, 1)
-            project(n + 2, 1, ("s1", "s2")[n])
-            turn_h(n)
-            gather_h(n)
-        spread(4)
-        interleave_err(3, nc.scalar.copy)
+        start_banks = ("mm1", "mm2")
+        for half in range(2):
+            for n in range(2):
+                project(n, half, start_banks[n])
+        for half in range(2):
+            for n in range(2):
+                weigh(n, half)
+                project(n + 2, half, start_banks[n])
+                if half == 1:
+                    turn_h(n)
+                    gather_h(n)
+        spread_weight(1)
+        interleave_err(0, 1, 1, nc.scalar.copy)
         weigh(2, 0)
         weigh(3, 0)
         project(LEAD, 0)
@@ -350,115 +369,120 @@ def tile_grouped_unembedding_gradient_k7_kernel(
         turn_h(2)
         project(LEAD, 1)
         turn_h(3)
-        quantize_err(0, both)
-        quantize_h(0, both)
+        quantize_err(0, 0)
+        quantize_h(0)
         gradient(0, 0)
-        interleave_err(2, nc.vector.tensor_copy)
+        interleave_err(0, 1, 0, nc.vector.tensor_copy)
         gather_h(2)
         gather_h(3)
-        gather_weight(1, nc.vector.tensor_copy)
-        quantize_err(1, both)
+        gather_weight(1, nc.scalar.copy)
+        quantize_err(0, 1)
         gradient(0, 1)
-        quantize_h(1, both)
+        quantize_h(2)
         for h in range(1, G):
-            spread(RATE_ROW + 4 * h)
+            spread_rate(h)
 
-        last = UNITS - 1
-        for s in range(0, UNITS - LEAD, 2):
+        for s in range(0, TILES - LEAD, 2):
             ahead = s + LEAD
-            if s % TILES == 0 and s // TILES + 2 < G:
-                load_err(s // TILES + 2, 0, whole)
-                load_stage1(s // TILES + 2)
-                load_err(s // TILES + 2, 1, whole)
-            load_running(s + 4)
-            interleave_err(ahead, nc.scalar.copy)
-            interleave_err(ahead + 1, nc.scalar.copy)
+            head, err_half = s // HEAD_TILES, s % HEAD_TILES // 2
+            last_round = ahead + 2 == TILES
+            if err_half == 0 and head + 2 < G:
+                load_err(head + 2, 0, whole)
+                load_a_words(head + 2)
+                load_err(head + 2, 1, whole)
+            if s == 0:
+                load_a_scales(slice(2, G))
+            load_running(ahead)
+            for g in range(2):
+                interleave_err(head + 1, err_half, g, nc.scalar.copy)
             if s == 0:
                 for h in range(1, G):
                     gather_rate(h, nc.scalar.copy)
-            for n in (s, s + 1):
-                for half in range(2):
-                    add_running(n, half)
-                    scale(n, halves[half], nc.gpsimd)
-                    if n == s or half == 0:
-                        gradient(n + 1, half)
-                store_y(n, whole)
-                if n == s:
-                    load_running(s + 5)
-                    for half in range(2):
-                        weigh(ahead, half)
-                        project(ahead + 1, half)
-            if s >= 2:
-                turn_y(s - 2, both)
-                turn_y(s - 1, both)
             else:
-                spread(8)
-                spread(12)
+                turn_y(s - 2, both_groups)
+
+            for half in range(2):
+                add_running(s, half)
+                scale(s, half, nc.gpsimd)
+                gradient(s + 1, half)
+            store_y(s, whole)
+            load_running(ahead + 1)
+            for half in range(2):
+                weigh(ahead, half)
+                project(ahead + 1, half)
+            add_running(s + 1, 0)
+            scale(s + 1, 0, nc.gpsimd)
+            gradient(s + 2, 0)
+            add_running(s + 1, 1)
+            if s == 0:
+                spread_weight(2)
+                spread_weight(3)
+            else:
+                turn_y(s - 1, both_groups)
             weigh(ahead + 1, 0)
-            if ahead + 2 < UNITS:
+            if not last_round:
                 project(ahead + 2, 0)
             weigh(ahead + 1, 1)
-            if s >= 2:
-                gather_y(s - 2, both, nc.vector.tensor_copy)
-                gather_y(s - 1, both, nc.vector.tensor_copy)
-            else:
+            if s == 0:
                 gather_weight(2, nc.vector.tensor_copy)
                 gather_weight(3, nc.vector.tensor_copy)
+            else:
+                gather_y(s - 2, both_groups, nc.vector.tensor_copy)
+                gather_y(s - 1, both_groups, nc.vector.tensor_copy)
+
+            scale(s + 1, 1, nc.vector)
+            store_y(s + 1, whole)
             turn_h(ahead)
             turn_h(ahead + 1)
-            if ahead + 2 < UNITS:
-                project(ahead + 2, 1)
+            if last_round:
+                gradient(s + 3, 0, "mm1")
             else:
-                gradient(s + 3, 0, "s1")
+                project(ahead + 2, 1)
             gather_h(ahead)
             gather_h(ahead + 1)
-            round_y(s, both, nc.scalar.copy)
-            if s >= TILES:
-                round_y(s + 1, both, nc.scalar.copy)
-            quantize_err(ahead // 2, both)
+            round_y(s, both_groups, nc.scalar.copy)
+            round_y(s + 1, both_groups, nc.scalar.copy)
+            quantize_err(head + 1, err_half)
             gradient(s + 2, 1)
-            if ahead + 2 == UNITS:
-                gradient(s + 3, 1, "s1")
-            if s >= TILES:
-                h, g = (s - TILES) // TILES, s % TILES // 2
-                quantize_y(h, g, slice(0, D))
-                store_codes(h, slice(g, g + 1), slice(0, D))
-            else:
-                round_y(s + 1, both, nc.vector.tensor_copy)
-            quantize_h(ahead // 2, both)
+            if last_round:
+                gradient(s + 3, 1, "mm1")
+            if head >= 1:
+                quantize_y(head - 1, err_half)
+                if err_half == 1:
+                    store_scales(head - 1, nc.sync)
+            quantize_h(ahead)
 
-        h = G - 1
-        base = UNITS - LEAD
+        base = TILES - LEAD
         order = [(n + j, half) for n in (base, base + 2) for half in range(2) for j in range(2)]
-        groups = (first, second)
-        turn_y(base - 2, both)
-        turn_y(base - 1, both)
-        gather_y(base - 2, both, nc.scalar.copy)
-        gather_y(base - 1, both, nc.scalar.copy)
+        for n in (base - 2, base - 1):
+            turn_y(n, both_groups)
+        for n in (base - 2, base - 1):
+            gather_y(n, both_groups, nc.scalar.copy)
         for i, (n, half) in enumerate(order):
             add_running(n, half)
-            if i < GPSIMD_HALVES:
-                scale(n, halves[half], nc.gpsimd)
+            if i < GPSIMD_LAST_HALVES:
+                scale(n, half, nc.gpsimd)
                 store_y(n, halves[half])
             if i + 4 < len(order):
-                gradient(*order[i + 4], ("s2", "s1")[i % 2])
-        for g in range(2):
-            quantize_y(h - 1, g, slice(0, D))
-        store_codes(h - 1, both, slice(0, D))
+                gradient(*order[i + 4], ("mm2", "mm1")[n % 2])
         for i, (n, half) in enumerate(order):
-            if i >= GPSIMD_HALVES:
-                scale(n, halves[half])
+            if i >= GPSIMD_LAST_HALVES:
+                scale(n, half, nc.vector)
                 store_y(n, halves[half])
-            round_y(n, groups[half], nc.scalar.copy if i < SCALAR_ROUNDS else nc.vector.tensor_copy)
-            turn_y(n, groups[half])
-            if i >= 1:
-                gather_y(order[i - 1][0], groups[order[i - 1][1]], nc.scalar.copy)
-        store_scales(slice(0, D * (G - 1)))
-        quantize_y(h, 0, slice(0, D))
-        gather_y(last, second, nc.scalar.copy)
-        quantize_y(h, 1, slice(0, 2 * P))
-        store_codes(h, first, slice(0, D))
-        quantize_y(h, 1, slice(2 * P, 3 * P))
-        quantize_y(h, 1, slice(3 * P, 4 * P))
-        store_codes(h, second, slice(0, D))
-        store_scales(slice(D * (G - 1), G * D))
+            if i in (3, 5):
+                quantize_y(G - 2, i // 2 - 1)
+            if i == 5:
+                store_scales(G - 2, nc.sync)
+            if i < len(order) - 2:
+                round_y(n, one_group[half], nc.scalar.copy)
+                turn_y(n, one_group[half])
+            if 1 <= i < len(order) - 1:
+                before, before_half = order[i - 1]
+                gather_y(before, one_group[before_half], nc.scalar.copy)
+        for n, half in order[-2:]:
+            round_y(n, one_group[half], nc.vector.tensor_copy)
+            turn_y(n, one_group[half])
+            gather_y(n, one_group[half], nc.scalar.copy)
+        for g in range(2):
+            quantize_y(G - 1, g)
+        store_scales(G - 1, nc.scalar)

from contextlib import ExitStack

import concourse.mybir as mybir
from concourse.masks import make_identity

G, T, K, D, V = 4, 1024, 1024, 512, 1024
BETA = 0.9
FLOPS = 2 * G * (T * K * D + T * D * V)

F32 = mybir.dt.float32
BF16 = mybir.dt.bfloat16
I32 = mybir.dt.int32
U32 = mybir.dt.uint32
U8 = mybir.dt.uint8
FP8X4 = mybir.dt.float8_e4m3fn_x4
FP4X4 = mybir.dt.float4_e2m1fn_x4
ADD = mybir.AluOpType.add
MULT = mybir.AluOpType.mult

P = 128
GROUP = 512
BANK = 512
PACK = 4
HEAD_TILES = D // P
TILES = G * HEAD_TILES
X_BLOCKS = T // P
LEAD = HEAD_TILES
VEC_ROWS = T // (2 * P)
RATE_ROW = 32
GPSIMD_LAST_HALVES = 2


def tile_grouped_unembedding_gradient_k7_kernel(
    tc, x, a_words, a_scales, bias, token_weight, err, running, rate, out_0, out_1, out_2
):
    nc = tc.nc
    with ExitStack() as ctx:
        keep = ctx.enter_context(tc.tile_pool(name="keep", bufs=1))
        work = ctx.enter_context(tc.tile_pool(name="work", bufs=2))
        psum = ctx.enter_context(tc.psum_pool(name="psum", bufs=2))
        ctx.enter_context(tc.manual_schedule())

        ident = keep.tile([P, P], F32, name="ident")
        bias_raw = keep.tile([TILES, P], BF16, name="bias_raw")
        bias_rows = keep.tile([P, P], F32, name="bias_rows")
        bias_cols = keep.tile([P, TILES], F32, name="bias_cols")
        vec_rows = keep.tile([P, P], F32, name="vec_rows")
        vec_cols = keep.tile([P, RATE_ROW + G * VEC_ROWS], F32, name="vec_cols")
        a_sc = keep.tile([P, 2 * G, D], U8, name="a_sc", align_bytes=64)
        x_codes = keep.tile([P, 2, T], U32, name="x_codes", align_bytes=64)
        x_sc = keep.tile([P, 2, T], U8, name="x_sc", align_bytes=64)

        x_raw, x_sorted, x_staged, a_w, weight_bc, rate_bc, spread_bank = {}, {}, {}, {}, {}, {}, {}
        run, e_raw, e_staged, e_codes, e_sc = {}, {}, {}, {}, {}
        mm1, h_t, h_bank, h_staged, h_codes, h_sc = {}, {}, {}, {}, {}, {}
        mm2, total, y, y_bf, y_bank, y_staged, y_codes, y_sc = {}, {}, {}, {}, {}, {}, {}, {}

        halves = (slice(0, BANK), slice(BANK, 2 * BANK))
        whole = slice(0, V)
        one_group = (slice(0, 1), slice(1, 2))
        both_groups = slice(0, 2)

        def transpose_bank(banks="tr"):
            return psum.tile([P, 4, P], F32, name=banks, bufs=4 if banks == "tr" else 2)


        def load_x(b):
            x_raw[b] = work.tile([P, K], BF16, name="x_raw", bufs=X_BLOCKS)
            nc.sync.dma_start(out=x_raw[b][:], in_=x[P * b : P * (b + 1), :])

        def load_a_words(h):
            a_w[h] = work.tile([P, 2, 2 * D], U8, name="a_w", bufs=2, align_bytes=64)
            words = a_words[2 * h : 2 * h + 2].rearrange("g p n -> p g n")
            nc.sync.dma_start(out=a_w[h][:].bitcast(I32), in_=words.bitcast(I32))

        def load_a_scales(heads):
            groups = slice(2 * heads.start, 2 * heads.stop)
            for quad in range(4):
                rows = a_scales[groups, 4 * quad : 4 * quad + 4, :].rearrange("g r n -> r g n")
                nc.sync.dma_start(out=a_sc[32 * quad : 32 * quad + 4, groups, :].bitcast(I32), in_=rows.bitcast(I32))

        def load_err(h, g, cols):
            raw = work.tile([P, PACK, cols.stop - cols.start], BF16, name="e_raw", bufs=4)
            rows = err[h, GROUP * g : GROUP * (g + 1), cols]
            nc.sync.dma_start(out=raw[:], in_=rows.rearrange("(p t) v -> p t v", t=PACK))
            for start in range(cols.start, cols.stop, BANK):
                e_raw[h, start // BANK, g] = raw[:, :, start - cols.start : start - cols.start + BANK]

        def load_running(n):
            h, j = divmod(n, HEAD_TILES)
            run[n] = work.tile([P, V], BF16, name="run", bufs=5)
            nc.sync.dma_start(out=run[n][:], in_=running[h, P * j : P * (j + 1), :])


        def spread(first_row, banks="tr"):
            spread_bank[first_row] = transpose_bank(banks)
            for q in range(VEC_ROWS):
                column = vec_cols[:, first_row + q : first_row + q + 1]
                nc.tensor.transpose(spread_bank[first_row][:, q, :], column.to_broadcast([P, P]), ident[:])

        def spread_weight(h, banks="tr"):
            spread(VEC_ROWS * h, banks)

        def spread_rate(h, banks="tr"):
            spread(RATE_ROW + VEC_ROWS * h, banks)

        def gather_weight(h, copy):
            weight_bc[h] = work.tile([P, T], BF16, name="weight_bc", bufs=G)
            pairs = spread_bank[VEC_ROWS * h][:].rearrange("c q w -> c (q w)")
            copy(
                out=weight_bc[h][:].bitcast(F32).rearrange("c (g u p) -> c g u p", g=2, u=2),
                in_=pairs.rearrange("c (g p u) -> c g u p", g=2, u=2),
            )

        def gather_rate(h, copy):
            rate_bc[h] = work.tile([P, V], BF16, name="rate_bc", bufs=G)
            pairs = spread_bank[RATE_ROW + VEC_ROWS * h][:].rearrange("c q w -> c (q w)")
            copy(out=rate_bc[h][:].bitcast(F32), in_=pairs)


        def sort_x(b):
            x_sorted[b] = work.tile([P, 4, P], F32, name="x_sorted", bufs=3)
            nc.vector.tensor_copy(
                out=x_sorted[b][:].rearrange("r (g u) p -> r g u p", u=2),
                in_=x_raw[b][:].bitcast(F32).rearrange("r (g p u) -> r g u p", g=2, u=2),
            )

        def turn_x(b):
            half, j = divmod(b, 4)
            if j == 0:
                x_staged[half] = work.tile([P, 2, BANK * PACK], BF16, name="staged", bufs=3, align_bytes=64)
            bank = transpose_bank()
            for q in range(4):
                nc.tensor.transpose(bank[:, q, :], x_sorted[b][:, q, :], ident[:])
            dst = x_staged[half][:].bitcast(F32).rearrange("c g (u j m e w) -> c g j u m e w", u=2, j=4, e=2, w=2)
            src = bank[:].rearrange("c (g w) (m u e) -> c g u m e w", w=2, u=2, e=2)
            for g in range(2):
                nc.scalar.copy(out=dst[:, g, j], in_=src[:, g])

        def quantize_x(half, g):
            nc.vector.quantize_mx(
                out=x_codes[:, g, halves[half]].bitcast(FP8X4),
                scales=x_sc[:, g, halves[half]],
                in_=x_staged[half][:, g, :],
            )


        def interleave_err(h, half, g, copy):
            if (h, half) not in e_staged:
                e_staged[h, half] = work.tile([P, 2, BANK * PACK], BF16, name="staged", bufs=3, align_bytes=64)
            copy(
                out=e_staged[h, half][:, g, :].rearrange("p (c i t) -> p c t i", i=4, t=PACK),
                in_=e_raw[h, half, g].rearrange("p t (c i) -> p c t i", i=4),
            )

        def quantize_err(h, half):
            e_codes[h, half] = work.tile([P, 2, BANK], U32, name="e_codes", bufs=4, align_bytes=64)
            e_sc[h, half] = work.tile([P, 2, BANK], U8, name="e_sc", bufs=4, align_bytes=64)
            nc.vector.quantize_mx(
                out=e_codes[h, half][:].rearrange("p g c -> p (g c)").bitcast(FP8X4),
                scales=e_sc[h, half][:].rearrange("p g c -> p (g c)"),
                in_=e_staged[h, half][:].rearrange("p g c -> p (g c)"),
            )


        def project(n, half, banks="mm1"):
            h, j = divmod(n, HEAD_TILES)
            mm1[n, half] = psum.tile([P, BANK], F32, name=banks, bufs=2)
            for g in range(2):
                nc.tensor.matmul_mx(
                    out=mm1[n, half][:],
                    lhsT=a_w[h][:, g, 2 * P * j : 2 * P * (j + 1)].bitcast(FP4X4),
                    lhsT_scale=a_sc[:, 2 * h + g, P * j : P * (j + 1)],
                    rhs=x_codes[:, g, halves[half]].bitcast(FP8X4),
                    rhs_scale=x_sc[:, g, halves[half]],
                    start=(g == 0),
                    stop=(g == 1),
                )

        def weigh(n, half):
            if half == 0:
                h_t[n] = work.tile([P, T], BF16, name="h_t", bufs=LEAD)
            nc.vector.scalar_tensor_tensor(
                out=h_t[n][:, halves[half]],
                in0=mm1[n, half][:],
                scalar=bias_cols[:, n : n + 1],
                in1=weight_bc[n // HEAD_TILES][:, halves[half]],
                op0=ADD,
                op1=MULT,
            )

        def turn_h(n):
            pairs = h_t[n][:].bitcast(F32)
            h_bank[n] = transpose_bank()
            for q in range(4):
                nc.tensor.transpose(h_bank[n][:, q, :], pairs[:, P * q : P * (q + 1)], ident[:])

        def gather_h(n):
            if n % 2 == 0:
                h_staged[n // 2] = work.tile([P, 2, T], BF16, name="h_staged", bufs=2, align_bytes=64)
            nc.scalar.copy(
                out=h_staged[n // 2][:, n % 2, :].bitcast(F32).rearrange("p (g d u) -> p g d u", g=2, u=2),
                in_=h_bank[n][:].rearrange("p (g u) d -> p g d u", u=2),
            )

        def quantize_h(n):
            couple = n // 2
            h_codes[couple] = work.tile([P, 2, 2 * P], U32, name="h_codes", bufs=3, align_bytes=64)
            h_sc[couple] = work.tile([P, 2, 2 * P], U8, name="h_sc", bufs=3, align_bytes=64)
            nc.vector.quantize_mx(
                out=h_codes[couple][:].rearrange("p j c -> p (j c)").bitcast(FP8X4),
                scales=h_sc[couple][:].rearrange("p j c -> p (j c)"),
                in_=h_staged[couple][:].rearrange("p j c -> p (j c)"),
            )


        def gradient(n, half, banks="mm2"):
            h = n // HEAD_TILES
            mm2[n, half] = psum.tile([P, BANK], F32, name=banks, bufs=2)
            for g in range(2):
                nc.tensor.matmul_mx(
                    out=mm2[n, half][:],
                    lhsT=h_codes[n // 2][:, n % 2, P * g : P * (g + 1)].bitcast(FP8X4),
                    lhsT_scale=h_sc[n // 2][:, n % 2, P * g : P * (g + 1)],
                    rhs=e_codes[h, half][:, g, :].bitcast(FP8X4),
                    rhs_scale=e_sc[h, half][:, g, :],
                    start=(g == 0),
                    stop=(g == 1),
                )

        def add_running(n, half):
            if half == 0:
                total[n] = work.tile([P, V], F32, name="total", bufs=HEAD_TILES)
            nc.vector.scalar_tensor_tensor(
                out=total[n][:, halves[half]],
                in0=run[n][:, halves[half]],
                scalar=BETA,
                in1=mm2[n, half][:],
                op0=MULT,
                op1=ADD,
            )

        def scale(n, half, engine):
            if half == 0:
                y[n] = work.tile([P, V], F32, name="y", bufs=HEAD_TILES)
            cols = halves[half]
            engine.tensor_tensor(
                out=y[n][:, cols], in0=total[n][:, cols], in1=rate_bc[n // HEAD_TILES][:, cols], op=MULT
            )

        def store_y(n, cols):
            h, j = divmod(n, HEAD_TILES)
            nc.sync.dma_start(out=out_0[h, P * j : P * (j + 1), cols], in_=y[n][:, cols])


        def round_y(n, groups, copy):
            if groups.start == 0:
                y_bf[n] = work.tile([P, V], BF16, name="y_bf", bufs=HEAD_TILES)
            copy(
                out=y_bf[n][:].rearrange("d (g u p e) -> d g u p e", g=2, u=2, e=2)[:, groups],
                in_=y[n][:].rearrange("d (g p u e) -> d g u p e", g=2, u=2, e=2)[:, groups],
            )

        def turn_y(n, groups):
            pairs = y_bf[n][:].bitcast(F32)
            y_bank[n, groups.start] = transpose_bank()
            for q in range(2 * groups.start, 2 * groups.stop):
                nc.tensor.transpose(y_bank[n, groups.start][:, q, :], pairs[:, P * q : P * (q + 1)], ident[:])

        def gather_y(n, groups, copy):
            h, j = divmod(n, HEAD_TILES)
            if j == 0 and groups.start == 0:
                y_staged[h] = work.tile([P, 2 * D * PACK], BF16, name="y_staged", bufs=2, align_bytes=64)
            dst = y_staged[h][:].bitcast(F32).rearrange("p (g d u) -> p g d u", g=2, u=2)
            copy(
                out=dst[:, groups, P * j : P * (j + 1), :],
                in_=y_bank[n, groups.start][:].rearrange("p (g u) d -> p g d u", u=2)[:, groups],
            )

        def quantize_y(h, g):
            if g == 0:
                y_sc[h] = work.tile([P, 2 * D], U8, name="y_sc", bufs=2, align_bytes=64)
            y_codes[h, g] = work.tile([P, D], U32, name="y_codes", bufs=4, align_bytes=64)
            nc.vector.quantize_mx(
                out=y_codes[h, g][:].bitcast(FP8X4),
                scales=y_sc[h][:, D * g : D * (g + 1)],
                in_=y_staged[h][:, PACK * D * g : PACK * D * (g + 1)],
            )
            rows = out_1[g].rearrange("p m t -> p (m t)")[:, PACK * D * h : PACK * D * (h + 1)]
            nc.sync.dma_start(out=rows.bitcast(I32), in_=y_codes[h, g][:].bitcast(I32))

        def store_scales(h, queue):
            for quad in range(4):
                rows = out_2[:, 4 * quad : 4 * quad + 4, D * h : D * (h + 1)].rearrange("g r m -> r g m")
                live = y_sc[h][32 * quad : 32 * quad + 4, :].bitcast(I32).rearrange("r (g m) -> r g m", g=2)
                queue.dma_start(out=rows.bitcast(I32), in_=live)


        nc.vector.memset(vec_rows[:], 0.0)
        nc.vector.memset(bias_rows[:], 0.0)
        nc.vector.memset(a_sc[:].bitcast(I32), 0)
        make_identity(nc, ident[:])
        for first_row, vec in ((0, token_weight), (RATE_ROW, rate)):
            nc.sync.dma_start(
                out=vec_rows[first_row : first_row + G * VEC_ROWS, :].bitcast(BF16),
                in_=vec.rearrange("h (q w) -> (h q) w", q=VEC_ROWS),
            )
        nc.sync.dma_start(out=bias_raw[:], in_=bias.rearrange("h (j p) -> (h j) p", p=P))
        for b in range(X_BLOCKS):
            load_x(b)
        load_a_scales(slice(0, 1))
        load_a_words(0)
        for half in range(2):
            for g in range(2):
                load_err(0, g, halves[half])
        load_running(0)
        load_a_words(1)
        load_a_scales(slice(1, 2))
        load_running(1)

        vec_bank = transpose_bank()
        nc.tensor.transpose(vec_bank[:, 0, :], vec_rows[:], ident[:])
        nc.vector.tensor_copy(out=vec_cols[:], in_=vec_bank[:, 0, : RATE_ROW + G * VEC_ROWS])
        nc.vector.tensor_copy(out=bias_rows[:TILES, :], in_=bias_raw[:])
        spread_weight(0, "mm1")
        sort_x(0)
        turn_x(0)
        bias_bank = transpose_bank()
        nc.tensor.transpose(bias_bank[:, 0, :], bias_rows[:], ident[:])
        sort_x(1)
        turn_x(1)
        gather_weight(0, nc.vector.tensor_copy)
        nc.vector.tensor_copy(out=bias_cols[:], in_=bias_bank[:, 0, :TILES])
        for b in range(2, X_BLOCKS):
            sort_x(b)
            if b == X_BLOCKS - 2:
                spread_rate(0, "mm2")
            turn_x(b)
        quantize_x(0, 0)
        quantize_x(0, 1)
        gather_rate(0, nc.vector.tensor_copy)
        quantize_x(1, 0)
        quantize_x(1, 1)

        interleave_err(0, 0, 0, nc.scalar.copy)
        load_err(1, 0, whole)
        load_running(2)
        load_running(3)
        interleave_err(0, 0, 1, nc.scalar.copy)
        load_err(1, 1, whole)
        start_banks = ("mm1", "mm2")
        for half in range(2):
            for n in range(2):
                project(n, half, start_banks[n])
        for half in range(2):
            for n in range(2):
                weigh(n, half)
                project(n + 2, half, start_banks[n])
                if half == 1:
                    turn_h(n)
                    gather_h(n)
        spread_weight(1)
        interleave_err(0, 1, 1, nc.scalar.copy)
        weigh(2, 0)
        weigh(3, 0)
        project(LEAD, 0)
        weigh(2, 1)
        weigh(3, 1)
        turn_h(2)
        project(LEAD, 1)
        turn_h(3)
        quantize_err(0, 0)
        quantize_h(0)
        gradient(0, 0)
        interleave_err(0, 1, 0, nc.vector.tensor_copy)
        gather_h(2)
        gather_h(3)
        gather_weight(1, nc.scalar.copy)
        quantize_err(0, 1)
        gradient(0, 1)
        quantize_h(2)
        for h in range(1, G):
            spread_rate(h)

        for s in range(0, TILES - LEAD, 2):
            ahead = s + LEAD
            head, err_half = s // HEAD_TILES, s % HEAD_TILES // 2
            last_round = ahead + 2 == TILES
            if err_half == 0 and head + 2 < G:
                load_err(head + 2, 0, whole)
                load_a_words(head + 2)
                load_err(head + 2, 1, whole)
            if s == 0:
                load_a_scales(slice(2, G))
            load_running(ahead)
            for g in range(2):
                interleave_err(head + 1, err_half, g, nc.scalar.copy)
            if s == 0:
                for h in range(1, G):
                    gather_rate(h, nc.scalar.copy)
            else:
                turn_y(s - 2, both_groups)

            for half in range(2):
                add_running(s, half)
                scale(s, half, nc.gpsimd)
                gradient(s + 1, half)
            store_y(s, whole)
            load_running(ahead + 1)
            for half in range(2):
                weigh(ahead, half)
                project(ahead + 1, half)
            add_running(s + 1, 0)
            scale(s + 1, 0, nc.gpsimd)
            gradient(s + 2, 0)
            add_running(s + 1, 1)
            if s == 0:
                spread_weight(2)
                spread_weight(3)
            else:
                turn_y(s - 1, both_groups)
            weigh(ahead + 1, 0)
            if not last_round:
                project(ahead + 2, 0)
            weigh(ahead + 1, 1)
            if s == 0:
                gather_weight(2, nc.vector.tensor_copy)
                gather_weight(3, nc.vector.tensor_copy)
            else:
                gather_y(s - 2, both_groups, nc.vector.tensor_copy)
                gather_y(s - 1, both_groups, nc.vector.tensor_copy)

            scale(s + 1, 1, nc.vector)
            store_y(s + 1, whole)
            turn_h(ahead)
            turn_h(ahead + 1)
            if last_round:
                gradient(s + 3, 0, "mm1")
            else:
                project(ahead + 2, 1)
            gather_h(ahead)
            gather_h(ahead + 1)
            round_y(s, both_groups, nc.scalar.copy)
            round_y(s + 1, both_groups, nc.scalar.copy)
            quantize_err(head + 1, err_half)
            gradient(s + 2, 1)
            if last_round:
                gradient(s + 3, 1, "mm1")
            if head >= 1:
                quantize_y(head - 1, err_half)
                if err_half == 1:
                    store_scales(head - 1, nc.sync)
            quantize_h(ahead)

        base = TILES - LEAD
        order = [(n + j, half) for n in (base, base + 2) for half in range(2) for j in range(2)]
        for n in (base - 2, base - 1):
            turn_y(n, both_groups)
        for n in (base - 2, base - 1):
            gather_y(n, both_groups, nc.scalar.copy)
        for i, (n, half) in enumerate(order):
            add_running(n, half)
            if i < GPSIMD_LAST_HALVES:
                scale(n, half, nc.gpsimd)
                store_y(n, halves[half])
            if i + 4 < len(order):
                gradient(*order[i + 4], ("mm2", "mm1")[n % 2])
        for i, (n, half) in enumerate(order):
            if i >= GPSIMD_LAST_HALVES:
                scale(n, half, nc.vector)
                store_y(n, halves[half])
            if i in (3, 5):
                quantize_y(G - 2, i // 2 - 1)
            if i == 5:
                store_scales(G - 2, nc.sync)
            if i < len(order) - 2:
                round_y(n, one_group[half], nc.scalar.copy)
                turn_y(n, one_group[half])
            if 1 <= i < len(order) - 1:
                before, before_half = order[i - 1]
                gather_y(before, one_group[before_half], nc.scalar.copy)
        for n, half in order[-2:]:
            round_y(n, one_group[half], nc.vector.tensor_copy)
            turn_y(n, one_group[half])
            gather_y(n, one_group[half], nc.scalar.copy)
        for g in range(2):
            quantize_y(G - 1, g)
        store_scales(G - 1, nc.scalar)
